import numpy as np
import ml_dtypes


def mxq(x, axis, fmt="e4m3"):
    dtype, down = {"e4m3": (ml_dtypes.float8_e4m3fn, 7), "e5m2": (ml_dtypes.float8_e5m2, 14)}[fmt]
    v = np.moveaxis(np.asarray(x, np.float32).astype(ml_dtypes.bfloat16).astype(np.float64), axis, -1)
    blocks = v.reshape(v.shape[:-1] + (-1, 32))
    amax = np.abs(blocks).max(-1, keepdims=True)
    byte = np.maximum(np.where(amax > 0, np.frexp(amax)[1] - 1 + 127, 0) - down, 1)
    scale = np.exp2(byte - 127.0)
    codes = (blocks / scale).astype(np.float32).astype(dtype).astype(np.float64)
    return np.moveaxis((codes * scale).reshape(v.shape), -1, axis)


WIDE = False


def mx_kscale(k):
    if not WIDE:
        return np.ones(k)
    levels = np.array([30, -30])
    if k % 512:
        return np.exp2(np.random.permutation(np.resize(levels, k // 32))).repeat(32)
    a = np.empty((k // 512, 16))
    for p in range(k // 512):
        a[p, :8] = np.random.permutation(np.resize(levels, 8))
        for g in range(8):
            far = levels[np.abs(levels - a[p, g]) >= 10]
            a[p, g + 8] = far[np.random.randint(len(far))]
    return np.exp2(a.ravel()).repeat(32)


def f64(x):
    return np.asarray(x).astype(np.float64)


def striped(idx):
    return np.tile(idx.reshape(-1, 16).T, (8, 1)).astype(np.uint16)


def unstriped(offs):
    return offs[:16].T.reshape(-1).astype(np.int64)


E2M1 = np.array([0.0, 0.5, 1.0, 1.5, 2.0, 3.0, 4.0, 6.0, -0.0, -0.5, -1.0, -1.5, -2.0, -3.0, -4.0, -6.0])


def pack_weight(w, fmt):
    k, n = w.shape
    w = f64(np.asarray(w, np.float32).astype(ml_dtypes.bfloat16)).reshape(k // 32, 32, n)
    amax = np.abs(w).max(1)
    if fmt == "e4m3":
        byte = np.frexp(amax)[1] - 1 + 127 - 7
    elif fmt == "e5m2":
        byte = np.frexp(amax)[1] - 1 + 127 - 14
    else:
        mant, ex = np.frexp(amax / 6.0)
        byte = np.where(mant > 0.5, ex, ex - 1) + 127
    byte = np.clip(np.where(amax > 0, byte, 1), 1, 254)
    scaled = (w * np.exp2(127.0 - byte)[:, None, :]).reshape(k, n).astype(np.float32)
    by_word = np.ascontiguousarray(scaled.reshape(k // 512, 128, 4, n).transpose(0, 1, 3, 2))
    if fmt == "e4m3":
        words = by_word.astype(ml_dtypes.float8_e4m3fn).view(np.uint8)
    elif fmt == "e5m2":
        words = by_word.astype(ml_dtypes.float8_e5m2).view(np.uint8)
    else:
        c = by_word.astype(ml_dtypes.float4_e2m1fn).view(np.uint8) & 0xF
        words = (c[..., 0::2] | (c[..., 1::2] << 4)).reshape(k // 512, 128, 2 * n)
    return np.ascontiguousarray(words), np.ascontiguousarray(byte.astype(np.uint8).reshape(k // 512, 16, n))


def unpack_weight(words, scales, fmt):
    g, _, n = scales.shape
    words = np.ascontiguousarray(words).reshape(g, 128, n, -1)
    if fmt == "e4m3":
        vals = words.view(ml_dtypes.float8_e4m3fn).astype(np.float64)
    elif fmt == "e5m2":
        vals = words.view(ml_dtypes.float8_e5m2).astype(np.float64)
    else:
        nib = np.empty((g, 128, n, 4), np.uint8)
        nib[..., 0::2] = words & 0xF
        nib[..., 1::2] = words >> 4
        vals = E2M1[nib]
    vals = vals * np.repeat(np.exp2(scales.astype(np.float64) - 127.0), 8, axis=1)[..., None]
    return vals.transpose(0, 1, 3, 2).reshape(g * 512, n)


def d_relu(v):
    return (v > 0).astype(np.float64)


K, T, E, C, H, N = 512, 1024, 2, 512, 512, 512


def by_expert(wq, xq):
    return np.concatenate([wq[e].T @ xq[:, e * C:(e + 1) * C] for e in range(E)], axis=1)


def setup_inputs():
    n = np.random.standard_normal
    v = mx_kscale(N)
    u = mx_kscale(H)
    slot_token = np.random.permutation(T)[:E * C]
    w_slot = np.random.uniform(0.2, 1.0, E * C)
    dy = pack_weight(n((N, T)) * v[:, None], "e5m2")
    w2t = pack_weight(n((N, H)) / np.sqrt(N) / v[:, None] * u, "e2m1")
    w1t = [pack_weight(m, "e2m1") for m in n((E, H, K)) / np.sqrt(H) / u[None, :, None]]
    return {
        "dy_words": dy[0],
        "dy_scales": dy[1],
        "w2t_words": w2t[0],
        "w2t_scales": w2t[1],
        "w1t_words": np.stack([m[0] for m in w1t]),
        "w1t_scales": np.stack([m[1] for m in w1t]),
        "a": (n((H, E * C))).astype(np.float32),
        "gate": (np.tile(w_slot, (128, 1))).astype(np.float32),
        "offs": striped(slot_token),
    }


def reference(dy_words, dy_scales, w2t_words, w2t_scales, w1t_words, w1t_scales, a, gate, offs):
    w2t = unpack_weight(w2t_words, w2t_scales, "e2m1")
    w1t = np.stack([unpack_weight(w1t_words[e], w1t_scales[e], "e2m1") for e in range(E)])
    idx = unstriped(offs)
    dc = w2t.T @ unpack_weight(dy_words, dy_scales, "e5m2")
    da = f64(gate[:1]) * dc[:, idx] * d_relu(f64(a))
    dx = by_expert(w1t, mxq(da, 0, "e5m2"))
    out = np.zeros((K, T))
    out[:, idx] = dx
    return out

@@ -1,0 +1,200 @@
+from contextlib import ExitStack
+
+import concourse.mybir as mybir
+
+K, T, E, C, H, N = 512, 1024, 2, 512, 512, 512
+FLOPS = 2 * N * H * T + 2 * H * K * E * C
+
+F32 = mybir.dt.float32
+BF16 = mybir.dt.bfloat16
+I32 = mybir.dt.int32
+U32 = mybir.dt.uint32
+U16 = mybir.dt.uint16
+U8 = mybir.dt.uint8
+E5M2X4 = mybir.dt.float8_e5m2_x4
+E2M1X4 = mybir.dt.float4_e2m1fn_x4
+ALU = mybir.AluOpType
+ACT = mybir.ActivationFunctionType
+
+P = 128
+PACK = 4
+BANK = 512
+HALF = C // 2
+LINE = 4
+
+
+def tile_moe_sdb_relu_kernel(
+    tc, dy_words, dy_scales, w2t_words, w2t_scales, w1t_words, w1t_scales, a, gate, offs, out
+):
+    nc = tc.nc
+    with ExitStack() as ctx:
+        sb = ctx.enter_context(tc.tile_pool(name="sb", bufs=1))
+        psum = ctx.enter_context(tc.psum_pool(name="psum", bufs=8))
+
+        offsets = sb.tile([P, E * C // 16], U16, name="offsets")
+        dy_w = sb.tile([P, T], U32, name="dy_w", align_bytes=64)
+        dy_s = sb.tile([P, T], U8, name="dy_s", align_bytes=64)
+        w2_raw_w = sb.tile([P, 2 * H], U8, name="w2_raw_w", align_bytes=64)
+        w2_raw_s = sb.tile([P, H], U8, name="w2_raw_s", align_bytes=64)
+        w2_w = sb.tile([P, 2 * H], U8, name="w2_w", align_bytes=64)
+        w2_s = sb.tile([P, H], U8, name="w2_s", align_bytes=64)
+        w1_w = sb.tile([P, E, 2 * K], U8, name="w1_w", align_bytes=64)
+        w1_s = sb.tile([P, E, K], U8, name="w1_s", align_bytes=64)
+        warm_in = sb.tile([P, 1], F32, name="warm_in")
+        warm_out = sb.tile([P, 1], F32, name="warm_out")
+        gate0 = sb.tile([P, C], F32, name="gate0", tag="after_first_gathers", align_bytes=64)
+        gate1 = sb.tile([P, C], F32, name="gate1")
+        gates = [gate0, gate1]
+        a_sb = [[sb.tile([P, PACK, HALF], F32, name="a%d%d" % (e, h)) for h in range(2)] for e in range(E)]
+        dc = [sb.tile([P, T], F32, name="dc%d" % t) for t in range(PACK)]
+        gated0 = sb.tile([P, PACK, C], F32, name="gated0")
+        shared = sb.tile([P, PACK, C], F32, name="shared", align_bytes=64)
+
+        def woven_tile(name, cols, tag=None):
+            return sb.tile([P, cols * PACK], BF16, name=name, tag=tag or name, align_bytes=64)[:]
+
+        signs = [[woven_tile("sign00", HALF), shared[:, 0, :].bitcast(BF16)], [woven_tile("sign10", HALF), woven_tile("sign11", HALF)]]
+        keeps = [[woven_tile("keep00", HALF), shared[:, 1, :].bitcast(BF16)], [woven_tile("keep10", HALF), woven_tile("keep11", HALF, "after_mask")]]
+        rounded = [[woven_tile("rounded%d%d" % (e, h), HALF) for h in range(2)] for e in range(E)]
+        da = [shared[:, 2:4, :].rearrange("p a c -> p (a c)").bitcast(BF16), woven_tile("da1", C, "after_quantise")]
+        da_w = [sb.tile([P, C], U32, name="da_w%d" % e, align_bytes=64) for e in range(E)]
+        da_s = [sb.tile([P, C], U8, name="da_s%d" % e, align_bytes=64) for e in range(E)]
+        dx = [[sb.tile([P, C], F32, name="dx%d%d" % (e, c)) for c in range(K // P)] for e in range(E)]
+
+        def quad(q):
+            return slice(32 * q, 32 * q + 4)
+
+        def rows(q):
+            return slice(4 * q, 4 * q + 4)
+
+        nc.vector.memset(w2_raw_s[:].bitcast(U32), 0)
+        nc.vector.memset(warm_in[:], 0.0)
+        for q in range(4):
+            eng = nc.scalar if q < 2 else nc.sync
+            eng.dma_start(out=dy_s[quad(q), :].bitcast(I32), in_=dy_scales[0, rows(q), :].bitcast(I32))
+        nc.sync.dma_start(out=w2_raw_w[:].bitcast(I32), in_=w2t_words[0].bitcast(I32))
+        nc.sync.dma_start(out=dy_w[:].bitcast(I32), in_=dy_words[0].rearrange("p t d -> p (t d)").bitcast(I32))
+        for q in range(4):
+            nc.sync.dma_start(out=w2_raw_s[quad(q), :].bitcast(I32), in_=w2t_scales[0, rows(q), :].bitcast(I32))
+        nc.scalar.activation(warm_out[:], warm_in[:], ACT.Sign)
+        nc.sync.dma_start(offsets[:], offs)
+        a_rows = a.rearrange("(p t) j -> p t j", t=PACK)
+        nc.sync.dma_start(out=gates[0][:], in_=gate[:, 0:C])
+        for h in range(2):
+            nc.sync.dma_start(out=a_sb[0][h][:], in_=a_rows[:, :, h * HALF : (h + 1) * HALF])
+        nc.sync.dma_start(out=gates[1][:], in_=gate[:, C : 2 * C])
+        nc.sync.dma_start(out=w1_w[:].bitcast(I32), in_=w1t_words[:, 0].rearrange("e p b -> p e b").bitcast(I32))
+        for q in range(4):
+            nc.sync.dma_start(
+                out=w1_s[quad(q), :, :].bitcast(I32),
+                in_=w1t_scales[:, 0, rows(q), :].rearrange("e r k -> r e k").bitcast(I32),
+            )
+        for h in range(2):
+            nc.sync.dma_start(out=a_sb[1][h][:], in_=a_rows[:, :, C + h * HALF : C + (h + 1) * HALF])
+
+        w_src = w2_raw_w[:].bitcast(U16).rearrange("p (m t) -> p t m", t=PACK)
+        w_dst = w2_w[:].bitcast(U16).rearrange("p (t m) -> p t m", t=PACK)
+        s_src = w2_raw_s[:].rearrange("p (m t) -> p t m", t=PACK)
+        s_dst = w2_s[:].rearrange("p (t m) -> p t m", t=PACK)
+        for ts in (slice(0, 1), slice(1, PACK)):
+            nc.vector.tensor_copy(out=w_dst[:, ts, :], in_=w_src[:, ts, :])
+            nc.vector.tensor_copy(out=s_dst[:, ts, :], in_=s_src[:, ts, :])
+
+        for t in range(PACK):
+            for b in range(T // BANK):
+                cols = slice(b * BANK, (b + 1) * BANK)
+                acc = psum.tile([P, BANK], F32, name="acc")
+                nc.tensor.matmul_mx(
+                    out=acc[:],
+                    lhsT=w2_w[:, 2 * P * t : 2 * P * (t + 1)].bitcast(E2M1X4),
+                    lhsT_scale=w2_s[:, P * t : P * (t + 1)],
+                    rhs=dy_w[:, cols].bitcast(E5M2X4),
+                    rhs_scale=dy_s[:, cols],
+                    start=True,
+                    stop=True,
+                )
+                if (t, b) == (0, 1):
+                    nc.vector.tensor_copy(out=dc[t][:, cols], in_=acc[:])
+                else:
+                    nc.scalar.copy(out=dc[t][:, cols], in_=acc[:])
+
+        def gather(dst, e, t, lo, hi):
+            lst = offsets[:, (e * C + lo) // 16 : (e * C + hi) // 16]
+            nc.vector.tensor_tensor(dst, dc[t][:].indirect(lst), gates[e][:, lo:hi], ALU.mult)
+
+        def woven(ap):
+            return ap.rearrange("p (c i t) -> p c t i", i=LINE, t=PACK)
+
+        def planes(ap):
+            return ap.rearrange("p t (c i) -> p c t i", i=LINE)
+
+        def sign(e, h):
+            nc.scalar.activation(woven(signs[e][h]), planes(a_sb[e][h][:]), ACT.Sign)
+
+        def round_once(e, h, src):
+            nc.scalar.copy(out=woven(rounded[e][h]), in_=planes(src))
+
+        def apply_mask(e, h):
+            cols = slice(h * HALF * PACK, (h + 1) * HALF * PACK)
+            nc.vector.tensor_tensor(da[e][:, cols], rounded[e][h], keeps[e][h], ALU.mult)
+
+        def quantise(e):
+            nc.vector.quantize_mx(out=da_w[e][:].bitcast(E5M2X4), scales=da_s[e][:], in_=da[e])
+
+        def expert(e):
+            for c in range(K // P):
+                acc = psum.tile([P, BANK], F32, name="acc")
+                nc.tensor.matmul_mx(
+                    out=acc[:],
+                    lhsT=w1_w[:, e, 2 * P * c : 2 * P * (c + 1)].bitcast(E2M1X4),
+                    lhsT_scale=w1_s[:, e, P * c : P * (c + 1)],
+                    rhs=da_w[e][:].bitcast(E5M2X4),
+                    rhs_scale=da_s[e][:],
+                    start=True,
+                    stop=True,
+                )
+                nc.scalar.copy(out=dx[e][c][:], in_=acc[:])
+
+        def scatter(e, c):
+            lst = offsets[:, e * C // 16 : (e + 1) * C // 16]
+            nc.vector.tensor_copy(res[c][:].indirect(lst), dx[e][c][:])
+
+        for t in range(PACK):
+            gather(gated0[:, t, :], 0, t, 0, C)
+        for h in range(2):
+            sign(0, h)
+        for h in range(2):
+            round_once(0, h, gated0[:, :, h * HALF : (h + 1) * HALF])
+        gated1 = sb.tile([P, PACK, HALF], F32, name="gated1", tag="after_first_gathers", align_bytes=64)
+        for t in range(PACK):
+            gather(gated1[:, t, :], 1, t, 0, HALF)
+        for h in range(2):
+            nc.vector.tensor_scalar(keeps[0][h], signs[0][h], 0.0, None, ALU.max)
+        gather(shared[:, 0, 0:HALF], 1, 0, HALF, C)
+        for h in range(2):
+            apply_mask(0, h)
+        gather(shared[:, 1, 0:HALF], 1, 1, HALF, C)
+        quantise(0)
+        expert(0)
+        for t in (2, 3):
+            gather(shared[:, t, 0:HALF], 1, t, HALF, C)
+        for h in range(2):
+            sign(1, h)
+        for h in range(2):
+            nc.scalar.activation(keeps[1][h], signs[1][h], ACT.Relu)
+        round_once(1, 0, gated1[:])
+        round_once(1, 1, shared[:, :, 0:HALF])
+        res = [sb.tile([P, T], F32, name="res%d" % c) for c in range(2)]
+        scatter(0, 0)
+        scatter(0, 1)
+        for h in range(2):
+            apply_mask(1, h)
+        res.append(sb.tile([P, T], F32, name="res2", tag="after_mask", align_bytes=64))
+        scatter(0, 2)
+        quantise(1)
+        expert(1)
+        res.append(sb.tile([P, T], F32, name="res3", tag="after_quantise", align_bytes=64))
+        scatter(0, 3)
+        for c in range(K // P):
+            scatter(1, c)
+            nc.sync.dma_start(out=out[c * P : (c + 1) * P, :], in_=res[c][:])

@@ -42,21 +42,25 @@ def tile_moe_sdb_relu_kernel(
         w1_s = sb.tile([P, E, K], U8, name="w1_s", align_bytes=64)
         warm_in = sb.tile([P, 1], F32, name="warm_in")
         warm_out = sb.tile([P, 1], F32, name="warm_out")
-        gate0 = sb.tile([P, C], F32, name="gate0", tag="after_first_gathers", align_bytes=64)
-        gate1 = sb.tile([P, C], F32, name="gate1")
-        gates = [gate0, gate1]
-        a_sb = [[sb.tile([P, PACK, HALF], F32, name="a%d%d" % (e, h)) for h in range(2)] for e in range(E)]
+        gates = [sb.tile([P, C], F32, name="gate%d" % e)[:] for e in range(E)]
+        shared = sb.tile([P, PACK * 2 * C + P], F32, name="shared", align_bytes=64)
+        gated0 = shared[:, 0 : PACK * C].rearrange("p (t c) -> p t c", t=PACK)
+        gated1 = shared[:, P:].rearrange("p (t c) -> p t c", t=PACK)[:, :, 0:C]
+        a00 = sb.tile([P, PACK, HALF], F32, name="a00")
+        a0 = [a00[:], shared[:, PACK * C : PACK * (C + HALF)].rearrange("p (t c) -> p t c", t=PACK)]
+        a1 = sb.tile([P, PACK, C], F32, name="a1")
         dc = [sb.tile([P, T], F32, name="dc%d" % t) for t in range(PACK)]
-        gated0 = sb.tile([P, PACK, C], F32, name="gated0")
-        shared = sb.tile([P, PACK, C], F32, name="shared", align_bytes=64)
 
         def woven_tile(name, cols, tag=None):
             return sb.tile([P, cols * PACK], BF16, name=name, tag=tag or name, align_bytes=64)[:]
 
-        signs = [[woven_tile("sign00", HALF), shared[:, 0, :].bitcast(BF16)], [woven_tile("sign10", HALF), woven_tile("sign11", HALF)]]
-        keeps = [[woven_tile("keep00", HALF), shared[:, 1, :].bitcast(BF16)], [woven_tile("keep10", HALF), woven_tile("keep11", HALF, "after_mask")]]
-        rounded = [[woven_tile("rounded%d%d" % (e, h), HALF) for h in range(2)] for e in range(E)]
-        da = [shared[:, 2:4, :].rearrange("p a c -> p (a c)").bitcast(BF16), woven_tile("da1", C, "after_quantise")]
+        sign0 = [woven_tile("sign0%d" % h, HALF) for h in range(2)]
+        keep0 = [woven_tile("keep0%d" % h, HALF) for h in range(2)]
+        rounded0 = [woven_tile("rounded0%d" % h, HALF) for h in range(2)]
+        sign1 = woven_tile("sign1", C)
+        keep1 = [woven_tile("keep1%d" % h, HALF) for h in range(2)]
+        rounded1 = [woven_tile("rounded10", HALF), woven_tile("rounded11", HALF, "after_mask")]
+        da = [woven_tile("da%d" % e, C) for e in range(E)]
         da_w = [sb.tile([P, C], U32, name="da_w%d" % e, align_bytes=64) for e in range(E)]
         da_s = [sb.tile([P, C], U8, name="da_s%d" % e, align_bytes=64) for e in range(E)]
         dx = [[sb.tile([P, C], F32, name="dx%d%d" % (e, c)) for c in range(K // P)] for e in range(E)]
@@ -69,28 +73,31 @@ def tile_moe_sdb_relu_kernel(
 
         nc.vector.memset(w2_raw_s[:].bitcast(U32), 0)
         nc.vector.memset(warm_in[:], 0.0)
-        for q in range(4):
-            eng = nc.scalar if q < 2 else nc.sync
+        def load_dy_scales(eng, q):
             eng.dma_start(out=dy_s[quad(q), :].bitcast(I32), in_=dy_scales[0, rows(q), :].bitcast(I32))
+
+        for q in (0, 1):
+            load_dy_scales(nc.sync, q)
         nc.sync.dma_start(out=w2_raw_w[:].bitcast(I32), in_=w2t_words[0].bitcast(I32))
-        nc.sync.dma_start(out=dy_w[:].bitcast(I32), in_=dy_words[0].rearrange("p t d -> p (t d)").bitcast(I32))
         for q in range(4):
             nc.sync.dma_start(out=w2_raw_s[quad(q), :].bitcast(I32), in_=w2t_scales[0, rows(q), :].bitcast(I32))
+        nc.sync.dma_start(out=dy_w[:].bitcast(I32), in_=dy_words[0].rearrange("p t d -> p (t d)").bitcast(I32))
+        for q in (2, 3):
+            load_dy_scales(nc.sync, q)
         nc.scalar.activation(warm_out[:], warm_in[:], ACT.Sign)
         nc.sync.dma_start(offsets[:], offs)
         a_rows = a.rearrange("(p t) j -> p t j", t=PACK)
-        nc.sync.dma_start(out=gates[0][:], in_=gate[:, 0:C])
+        nc.sync.dma_start(out=gates[0], in_=gate[:, 0:C])
         for h in range(2):
-            nc.sync.dma_start(out=a_sb[0][h][:], in_=a_rows[:, :, h * HALF : (h + 1) * HALF])
-        nc.sync.dma_start(out=gates[1][:], in_=gate[:, C : 2 * C])
+            nc.sync.dma_start(out=a0[h], in_=a_rows[:, :, h * HALF : (h + 1) * HALF])
+        nc.sync.dma_start(out=gates[1], in_=gate[:, C : 2 * C])
         nc.sync.dma_start(out=w1_w[:].bitcast(I32), in_=w1t_words[:, 0].rearrange("e p b -> p e b").bitcast(I32))
         for q in range(4):
             nc.sync.dma_start(
                 out=w1_s[quad(q), :, :].bitcast(I32),
                 in_=w1t_scales[:, 0, rows(q), :].rearrange("e r k -> r e k").bitcast(I32),
             )
-        for h in range(2):
-            nc.sync.dma_start(out=a_sb[1][h][:], in_=a_rows[:, :, C + h * HALF : C + (h + 1) * HALF])
+        nc.sync.dma_start(out=a1[:], in_=a_rows[:, :, C : 2 * C])
 
         w_src = w2_raw_w[:].bitcast(U16).rearrange("p (m t) -> p t m", t=PACK)
         w_dst = w2_w[:].bitcast(U16).rearrange("p (t m) -> p t m", t=PACK)
@@ -113,7 +120,7 @@ def tile_moe_sdb_relu_kernel(
                     start=True,
                     stop=True,
                 )
-                if (t, b) == (0, 1):
+                if t == 0:
                     nc.vector.tensor_copy(out=dc[t][:, cols], in_=acc[:])
                 else:
                     nc.scalar.copy(out=dc[t][:, cols], in_=acc[:])
@@ -127,16 +134,6 @@ def tile_moe_sdb_relu_kernel(
 
         def planes(ap):
             return ap.rearrange("p t (c i) -> p c t i", i=LINE)
-
-        def sign(e, h):
-            nc.scalar.activation(woven(signs[e][h]), planes(a_sb[e][h][:]), ACT.Sign)
-
-        def round_once(e, h, src):
-            nc.scalar.copy(out=woven(rounded[e][h]), in_=planes(src))
-
-        def apply_mask(e, h):
-            cols = slice(h * HALF * PACK, (h + 1) * HALF * PACK)
-            nc.vector.tensor_tensor(da[e][:, cols], rounded[e][h], keeps[e][h], ALU.mult)
 
         def quantise(e):
             nc.vector.quantize_mx(out=da_w[e][:].bitcast(E5M2X4), scales=da_s[e][:], in_=da[e])
@@ -162,38 +159,33 @@ def tile_moe_sdb_relu_kernel(
         for t in range(PACK):
             gather(gated0[:, t, :], 0, t, 0, C)
         for h in range(2):
-            sign(0, h)
+            nc.scalar.activation(woven(sign0[h]), planes(a0[h]), ACT.Sign)
         for h in range(2):
-            round_once(0, h, gated0[:, :, h * HALF : (h + 1) * HALF])
-        gated1 = sb.tile([P, PACK, HALF], F32, name="gated1", tag="after_first_gathers", align_bytes=64)
-        for t in range(PACK):
-            gather(gated1[:, t, :], 1, t, 0, HALF)
+            nc.scalar.copy(out=woven(rounded0[h]), in_=planes(gated0[:, :, h * HALF : (h + 1) * HALF]))
+        gather(gated1[:, 3, :], 1, 3, 0, C)
         for h in range(2):
-            nc.vector.tensor_scalar(keeps[0][h], signs[0][h], 0.0, None, ALU.max)
-        gather(shared[:, 0, 0:HALF], 1, 0, HALF, C)
+            nc.vector.tensor_scalar(keep0[h], sign0[h], 0.0, None, ALU.max)
+        gather(gated1[:, 2, :], 1, 2, 0, C)
         for h in range(2):
-            apply_mask(0, h)
-        gather(shared[:, 1, 0:HALF], 1, 1, HALF, C)
+            cols = slice(h * HALF * PACK, (h + 1) * HALF * PACK)
+            nc.vector.tensor_tensor(da[0][:, cols], rounded0[h], keep0[h], ALU.mult)
+        gather(gated1[:, 1, 0:HALF], 1, 1, 0, HALF)
         quantise(0)
         expert(0)
-        for t in (2, 3):
-            gather(shared[:, t, 0:HALF], 1, t, HALF, C)
+        gather(gated1[:, 1, HALF:C], 1, 1, HALF, C)
+        gather(gated1[:, 0, :], 1, 0, 0, C)
+        nc.scalar.activation(woven(sign1), planes(a1[:]), ACT.Sign)
         for h in range(2):
-            sign(1, h)
-        for h in range(2):
-            nc.scalar.activation(keeps[1][h], signs[1][h], ACT.Relu)
-        round_once(1, 0, gated1[:])
-        round_once(1, 1, shared[:, :, 0:HALF])
-        res = [sb.tile([P, T], F32, name="res%d" % c) for c in range(2)]
-        scatter(0, 0)
-        scatter(0, 1)
-        for h in range(2):
-            apply_mask(1, h)
-        res.append(sb.tile([P, T], F32, name="res2", tag="after_mask", align_bytes=64))
-        scatter(0, 2)
+            cols = slice(h * HALF * PACK, (h + 1) * HALF * PACK)
+            nc.scalar.activation(keep1[h], sign1[:, cols], ACT.Relu)
+            nc.scalar.copy(out=woven(rounded1[h]), in_=planes(gated1[:, :, h * HALF : (h + 1) * HALF]))
+            nc.gpsimd.tensor_tensor(da[1][:, cols], rounded1[h], keep1[h], ALU.mult)
+        res = [sb.tile([P, T], F32, name="res%d" % c) for c in range(3)]
+        for c in range(3):
+            scatter(0, c)
         quantise(1)
         expert(1)
-        res.append(sb.tile([P, T], F32, name="res3", tag="after_quantise", align_bytes=64))
+        res.append(sb.tile([P, T], F32, name="res3", tag="after_mask", align_bytes=64))
         scatter(0, 3)
         for c in range(K // P):
             scatter(1, c)

@@ -18,9 +18,12 @@ ACT = mybir.ActivationFunctionType
 
 P = 128
 PACK = 4
+QUADS = 4
 BANK = 512
+BANKS = 8
 HALF = C // 2
 LINE = 4
+PER_COLUMN = 16
 
 
 def tile_moe_sdb_relu_kernel(
@@ -29,9 +32,9 @@ def tile_moe_sdb_relu_kernel(
     nc = tc.nc
     with ExitStack() as ctx:
         sb = ctx.enter_context(tc.tile_pool(name="sb", bufs=1))
-        psum = ctx.enter_context(tc.psum_pool(name="psum", bufs=8))
+        psum = ctx.enter_context(tc.psum_pool(name="psum", bufs=BANKS))
 
-        offsets = sb.tile([P, E * C // 16], U16, name="offsets")
+        offsets = sb.tile([P, E * C // PER_COLUMN], U16, name="offsets")
         dy_w = sb.tile([P, T], U32, name="dy_w", align_bytes=64)
         dy_s = sb.tile([P, T], U8, name="dy_s", align_bytes=64)
         w2_raw_w = sb.tile([P, 2 * H], U8, name="w2_raw_w", align_bytes=64)
@@ -40,19 +43,18 @@ def tile_moe_sdb_relu_kernel(
         w2_s = sb.tile([P, H], U8, name="w2_s", align_bytes=64)
         w1_w = sb.tile([P, E, 2 * K], U8, name="w1_w", align_bytes=64)
         w1_s = sb.tile([P, E, K], U8, name="w1_s", align_bytes=64)
-        warm_in = sb.tile([P, 1], F32, name="warm_in")
-        warm_out = sb.tile([P, 1], F32, name="warm_out")
         gates = [sb.tile([P, C], F32, name="gate%d" % e)[:] for e in range(E)]
-        shared = sb.tile([P, PACK * 2 * C + P], F32, name="shared", align_bytes=64)
-        gated0 = shared[:, 0 : PACK * C].rearrange("p (t c) -> p t c", t=PACK)
-        gated1 = shared[:, P:].rearrange("p (t c) -> p t c", t=PACK)[:, :, 0:C]
-        a00 = sb.tile([P, PACK, HALF], F32, name="a00")
-        a0 = [a00[:], shared[:, PACK * C : PACK * (C + HALF)].rearrange("p (t c) -> p t c", t=PACK)]
+
+        reused = sb.tile([P, PACK * 2 * C + P], F32, name="reused", align_bytes=64)
+        gated0 = reused[:, 0 : PACK * C].rearrange("p (t c) -> p t c", t=PACK)
+        gated1 = reused[:, P:].rearrange("p (t c) -> p t c", t=PACK)[:, :, 0:C]
+        a0_first = sb.tile([P, PACK, HALF], F32, name="a0_first")
+        a0 = [a0_first[:], reused[:, PACK * C : PACK * (C + HALF)].rearrange("p (t c) -> p t c", t=PACK)]
         a1 = sb.tile([P, PACK, C], F32, name="a1")
         dc = [sb.tile([P, T], F32, name="dc%d" % t) for t in range(PACK)]
 
-        def woven_tile(name, cols, tag=None):
-            return sb.tile([P, cols * PACK], BF16, name=name, tag=tag or name, align_bytes=64)[:]
+        def woven_tile(name, slots, tag=None):
+            return sb.tile([P, slots * PACK], BF16, name=name, tag=tag or name, align_bytes=64)[:]
 
         sign0 = [woven_tile("sign0%d" % h, HALF) for h in range(2)]
         keep0 = [woven_tile("keep0%d" % h, HALF) for h in range(2)]
@@ -65,75 +67,82 @@ def tile_moe_sdb_relu_kernel(
         da_s = [sb.tile([P, C], U8, name="da_s%d" % e, align_bytes=64) for e in range(E)]
         dx = [[sb.tile([P, C], F32, name="dx%d%d" % (e, c)) for c in range(K // P)] for e in range(E)]
 
-        def quad(q):
+        def scale_partitions(q):
             return slice(32 * q, 32 * q + 4)
 
-        def rows(q):
+        def scale_rows(q):
             return slice(4 * q, 4 * q + 4)
 
-        nc.vector.memset(w2_raw_s[:].bitcast(U32), 0)
-        nc.vector.memset(warm_in[:], 0.0)
-        def load_dy_scales(eng, q):
-            eng.dma_start(out=dy_s[quad(q), :].bitcast(I32), in_=dy_scales[0, rows(q), :].bitcast(I32))
+        def load_dy_scales(q):
+            nc.sync.dma_start(
+                out=dy_s[scale_partitions(q), :].bitcast(I32), in_=dy_scales[0, scale_rows(q), :].bitcast(I32)
+            )
 
-        for q in (0, 1):
-            load_dy_scales(nc.sync, q)
+        nc.vector.memset(w2_raw_s[:].bitcast(U32), 0)
+        for q in range(QUADS // 2):
+            load_dy_scales(q)
         nc.sync.dma_start(out=w2_raw_w[:].bitcast(I32), in_=w2t_words[0].bitcast(I32))
-        for q in range(4):
-            nc.sync.dma_start(out=w2_raw_s[quad(q), :].bitcast(I32), in_=w2t_scales[0, rows(q), :].bitcast(I32))
         nc.sync.dma_start(out=dy_w[:].bitcast(I32), in_=dy_words[0].rearrange("p t d -> p (t d)").bitcast(I32))
-        for q in (2, 3):
-            load_dy_scales(nc.sync, q)
-        nc.scalar.activation(warm_out[:], warm_in[:], ACT.Sign)
-        nc.sync.dma_start(offsets[:], offs)
-        a_rows = a.rearrange("(p t) j -> p t j", t=PACK)
+        for q in range(QUADS):
+            nc.sync.dma_start(
+                out=w2_raw_s[scale_partitions(q), :].bitcast(I32), in_=w2t_scales[0, scale_rows(q), :].bitcast(I32)
+            )
+        for q in range(QUADS // 2, QUADS):
+            load_dy_scales(q)
+        a_planes = a.rearrange("(p t) j -> p t j", t=PACK)
         nc.sync.dma_start(out=gates[0], in_=gate[:, 0:C])
+        nc.sync.dma_start(offsets[:], offs)
         for h in range(2):
-            nc.sync.dma_start(out=a0[h], in_=a_rows[:, :, h * HALF : (h + 1) * HALF])
+            nc.sync.dma_start(out=a0[h], in_=a_planes[:, :, h * HALF : (h + 1) * HALF])
         nc.sync.dma_start(out=gates[1], in_=gate[:, C : 2 * C])
         nc.sync.dma_start(out=w1_w[:].bitcast(I32), in_=w1t_words[:, 0].rearrange("e p b -> p e b").bitcast(I32))
-        for q in range(4):
+        for q in range(QUADS):
             nc.sync.dma_start(
-                out=w1_s[quad(q), :, :].bitcast(I32),
-                in_=w1t_scales[:, 0, rows(q), :].rearrange("e r k -> r e k").bitcast(I32),
+                out=w1_s[scale_partitions(q), :, :].bitcast(I32),
+                in_=w1t_scales[:, 0, scale_rows(q), :].rearrange("e r k -> r e k").bitcast(I32),
             )
-        nc.sync.dma_start(out=a1[:], in_=a_rows[:, :, C : 2 * C])
+        nc.sync.dma_start(out=a1[:], in_=a_planes[:, :, C : 2 * C])
 
         w_src = w2_raw_w[:].bitcast(U16).rearrange("p (m t) -> p t m", t=PACK)
         w_dst = w2_w[:].bitcast(U16).rearrange("p (t m) -> p t m", t=PACK)
         s_src = w2_raw_s[:].rearrange("p (m t) -> p t m", t=PACK)
         s_dst = w2_s[:].rearrange("p (t m) -> p t m", t=PACK)
-        for ts in (slice(0, 1), slice(1, PACK)):
-            nc.vector.tensor_copy(out=w_dst[:, ts, :], in_=w_src[:, ts, :])
-            nc.vector.tensor_copy(out=s_dst[:, ts, :], in_=s_src[:, ts, :])
+        for some_planes in (slice(0, 1), slice(1, PACK)):
+            nc.vector.tensor_copy(out=w_dst[:, some_planes, :], in_=w_src[:, some_planes, :])
+            nc.vector.tensor_copy(out=s_dst[:, some_planes, :], in_=s_src[:, some_planes, :])
 
         for t in range(PACK):
             for b in range(T // BANK):
-                cols = slice(b * BANK, (b + 1) * BANK)
+                tokens = slice(b * BANK, (b + 1) * BANK)
                 acc = psum.tile([P, BANK], F32, name="acc")
                 nc.tensor.matmul_mx(
                     out=acc[:],
                     lhsT=w2_w[:, 2 * P * t : 2 * P * (t + 1)].bitcast(E2M1X4),
                     lhsT_scale=w2_s[:, P * t : P * (t + 1)],
-                    rhs=dy_w[:, cols].bitcast(E5M2X4),
-                    rhs_scale=dy_s[:, cols],
+                    rhs=dy_w[:, tokens].bitcast(E5M2X4),
+                    rhs_scale=dy_s[:, tokens],
                     start=True,
                     stop=True,
                 )
-                if t == 0:
-                    nc.vector.tensor_copy(out=dc[t][:, cols], in_=acc[:])
+                if (t, b) == (0, 0):
+                    nc.vector.tensor_copy(out=dc[t][:, tokens], in_=acc[:])
                 else:
-                    nc.scalar.copy(out=dc[t][:, cols], in_=acc[:])
+                    nc.scalar.activation(dc[t][:, tokens], acc[:], ACT.Copy)
 
-        def gather(dst, e, t, lo, hi):
-            lst = offsets[:, (e * C + lo) // 16 : (e * C + hi) // 16]
-            nc.vector.tensor_tensor(dst, dc[t][:].indirect(lst), gates[e][:, lo:hi], ALU.mult)
+        def entries(e, lo, hi):
+            return offsets[:, (e * C + lo) // PER_COLUMN : (e * C + hi) // PER_COLUMN]
+
+        def gather(gated, e, t, lo, hi):
+            nc.vector.tensor_tensor(gated[:, t, lo:hi], dc[t][:].indirect(entries(e, lo, hi)), gates[e][:, lo:hi], ALU.mult)
 
         def woven(ap):
             return ap.rearrange("p (c i t) -> p c t i", i=LINE, t=PACK)
 
         def planes(ap):
             return ap.rearrange("p t (c i) -> p c t i", i=LINE)
+
+        def woven_half(h):
+            return slice(h * HALF * PACK, (h + 1) * HALF * PACK)
 
         def quantise(e):
             nc.vector.quantize_mx(out=da_w[e][:].bitcast(E5M2X4), scales=da_s[e][:], in_=da[e])
@@ -153,40 +162,40 @@ def tile_moe_sdb_relu_kernel(
                 nc.scalar.copy(out=dx[e][c][:], in_=acc[:])
 
         def scatter(e, c):
-            lst = offsets[:, e * C // 16 : (e + 1) * C // 16]
-            nc.vector.tensor_copy(res[c][:].indirect(lst), dx[e][c][:])
+            nc.vector.tensor_copy(res[c][:].indirect(entries(e, 0, C)), dx[e][c][:])
 
         for t in range(PACK):
-            gather(gated0[:, t, :], 0, t, 0, C)
+            gather(gated0, 0, t, 0, C)
         for h in range(2):
             nc.scalar.activation(woven(sign0[h]), planes(a0[h]), ACT.Sign)
         for h in range(2):
             nc.scalar.copy(out=woven(rounded0[h]), in_=planes(gated0[:, :, h * HALF : (h + 1) * HALF]))
-        gather(gated1[:, 3, :], 1, 3, 0, C)
+        gather(gated1, 1, 3, 0, C)
         for h in range(2):
             nc.vector.tensor_scalar(keep0[h], sign0[h], 0.0, None, ALU.max)
-        gather(gated1[:, 2, :], 1, 2, 0, C)
+        gather(gated1, 1, 2, 0, C)
         for h in range(2):
-            cols = slice(h * HALF * PACK, (h + 1) * HALF * PACK)
-            nc.vector.tensor_tensor(da[0][:, cols], rounded0[h], keep0[h], ALU.mult)
-        gather(gated1[:, 1, 0:HALF], 1, 1, 0, HALF)
+            nc.vector.tensor_tensor(da[0][:, woven_half(h)], rounded0[h], keep0[h], ALU.mult)
+        gather(gated1, 1, 1, 0, HALF)
         quantise(0)
         expert(0)
-        gather(gated1[:, 1, HALF:C], 1, 1, HALF, C)
-        gather(gated1[:, 0, :], 1, 0, 0, C)
+        gather(gated1, 1, 1, HALF, C)
+        gather(gated1, 1, 0, 0, C)
+
         nc.scalar.activation(woven(sign1), planes(a1[:]), ACT.Sign)
         for h in range(2):
-            cols = slice(h * HALF * PACK, (h + 1) * HALF * PACK)
-            nc.scalar.activation(keep1[h], sign1[:, cols], ACT.Relu)
+            nc.scalar.activation(keep1[h], sign1[:, woven_half(h)], ACT.Relu)
             nc.scalar.copy(out=woven(rounded1[h]), in_=planes(gated1[:, :, h * HALF : (h + 1) * HALF]))
-            nc.gpsimd.tensor_tensor(da[1][:, cols], rounded1[h], keep1[h], ALU.mult)
-        res = [sb.tile([P, T], F32, name="res%d" % c) for c in range(3)]
-        for c in range(3):
+            nc.gpsimd.tensor_tensor(da[1][:, woven_half(h)], rounded1[h], keep1[h], ALU.mult)
+
+        last = K // P - 1
+        res = [sb.tile([P, T], F32, name="res%d" % c) for c in range(last)]
+        for c in range(last):
             scatter(0, c)
         quantise(1)
         expert(1)
-        res.append(sb.tile([P, T], F32, name="res3", tag="after_mask", align_bytes=64))
-        scatter(0, 3)
+        res.append(sb.tile([P, T], F32, name="res%d" % last, tag="after_mask", align_bytes=64))
+        scatter(0, last)
         for c in range(K // P):
             scatter(1, c)
             nc.sync.dma_start(out=out[c * P : (c + 1) * P, :], in_=res[c][:])

@@ -1,6 +1,7 @@
 from contextlib import ExitStack
 
 import concourse.mybir as mybir
+from concourse.masks import make_identity
 
 K, T, E, C, H, N = 512, 1024, 2, 512, 512, 512
 FLOPS = 2 * N * H * T + 2 * H * K * E * C
@@ -22,6 +23,7 @@ QUADS = 4
 BANK = 512
 BANKS = 8
 HALF = C // 2
+QUARTER = C // 4
 LINE = 4
 PER_COLUMN = 16
 
@@ -45,27 +47,29 @@ def tile_moe_sdb_relu_kernel(
         w1_s = sb.tile([P, E, K], U8, name="w1_s", align_bytes=64)
         gates = [sb.tile([P, C], F32, name="gate%d" % e)[:] for e in range(E)]
 
-        reused = sb.tile([P, PACK * 2 * C + P], F32, name="reused", align_bytes=64)
-        gated0 = reused[:, 0 : PACK * C].rearrange("p (t c) -> p t c", t=PACK)
-        gated1 = reused[:, P:].rearrange("p (t c) -> p t c", t=PACK)[:, :, 0:C]
-        a0_first = sb.tile([P, PACK, HALF], F32, name="a0_first")
-        a0 = [a0_first[:], reused[:, PACK * C : PACK * (C + HALF)].rearrange("p (t c) -> p t c", t=PACK)]
+        identity = sb.tile([P, P], F32, name="identity")
+        make_identity(nc, identity[:])
+        a0 = [sb.tile([P, PACK, HALF], F32, name="a0%d" % h) for h in range(2)]
         a1 = sb.tile([P, PACK, C], F32, name="a1")
         dc = [sb.tile([P, T], F32, name="dc%d" % t) for t in range(PACK)]
+        gated0 = sb.tile([P, PACK, C], F32, name="gated0", tag="after_mask0_a", align_bytes=64)
+
+        piece = QUARTER // 2
+        reused = sb.tile([P, piece + PACK * C], F32, name="reused", align_bytes=64)
+        raw1 = reused[:, piece:].rearrange("p (t c) -> p t c", t=PACK)
+        keep_first = reused[:, 0 : PACK * C].bitcast(BF16).rearrange("p (j x) -> p j x", j=PACK)[:, :, 0:QUARTER]
 
         def woven_tile(name, slots, tag=None):
             return sb.tile([P, slots * PACK], BF16, name=name, tag=tag or name, align_bytes=64)[:]
 
-        sign0 = [woven_tile("sign0%d" % h, HALF) for h in range(2)]
-        keep0 = [woven_tile("keep0%d" % h, HALF) for h in range(2)]
-        rounded0 = [woven_tile("rounded0%d" % h, HALF) for h in range(2)]
-        sign1 = woven_tile("sign1", C)
+        sign0 = [woven_tile("sign0%d" % u, QUARTER) for u in range(4)]
+        keep0 = [None] + [woven_tile("keep0%d" % u, QUARTER, "after_mask0_b" if u == 3 else None) for u in range(1, 4)]
+        da0 = woven_tile("da0", 3 * QUARTER, "after_quantise0")
         keep1 = [woven_tile("keep1%d" % h, HALF) for h in range(2)]
-        rounded1 = [woven_tile("rounded10", HALF), woven_tile("rounded11", HALF, "after_mask")]
-        da = [woven_tile("da%d" % e, C) for e in range(E)]
+        rounded1 = [woven_tile("rounded10", HALF), woven_tile("rounded11", HALF, "after_mask1")]
+        da1 = woven_tile("da1", C)
         da_w = [sb.tile([P, C], U32, name="da_w%d" % e, align_bytes=64) for e in range(E)]
         da_s = [sb.tile([P, C], U8, name="da_s%d" % e, align_bytes=64) for e in range(E)]
-        dx = [[sb.tile([P, C], F32, name="dx%d%d" % (e, c)) for c in range(K // P)] for e in range(E)]
 
         def scale_partitions(q):
             return slice(32 * q, 32 * q + 4)
@@ -93,7 +97,7 @@ def tile_moe_sdb_relu_kernel(
         nc.sync.dma_start(out=gates[0], in_=gate[:, 0:C])
         nc.sync.dma_start(offsets[:], offs)
         for h in range(2):
-            nc.sync.dma_start(out=a0[h], in_=a_planes[:, :, h * HALF : (h + 1) * HALF])
+            nc.sync.dma_start(out=a0[h][:], in_=a_planes[:, :, h * HALF : (h + 1) * HALF])
         nc.sync.dma_start(out=gates[1], in_=gate[:, C : 2 * C])
         nc.sync.dma_start(out=w1_w[:].bitcast(I32), in_=w1t_words[:, 0].rearrange("e p b -> p e b").bitcast(I32))
         for q in range(QUADS):
@@ -132,9 +136,6 @@ def tile_moe_sdb_relu_kernel(
         def entries(e, lo, hi):
             return offsets[:, (e * C + lo) // PER_COLUMN : (e * C + hi) // PER_COLUMN]
 
-        def gather(gated, e, t, lo, hi):
-            nc.vector.tensor_tensor(gated[:, t, lo:hi], dc[t][:].indirect(entries(e, lo, hi)), gates[e][:, lo:hi], ALU.mult)
-
         def woven(ap):
             return ap.rearrange("p (c i t) -> p c t i", i=LINE, t=PACK)
 
@@ -144,58 +145,118 @@ def tile_moe_sdb_relu_kernel(
         def woven_half(h):
             return slice(h * HALF * PACK, (h + 1) * HALF * PACK)
 
-        def quantise(e):
-            nc.vector.quantize_mx(out=da_w[e][:].bitcast(E5M2X4), scales=da_s[e][:], in_=da[e])
+        def quantise(e, lo, hi, values):
+            nc.vector.quantize_mx(out=da_w[e][:, lo:hi].bitcast(E5M2X4), scales=da_s[e][:, lo:hi], in_=values)
 
-        def expert(e):
-            for c in range(K // P):
-                acc = psum.tile([P, BANK], F32, name="acc")
-                nc.tensor.matmul_mx(
-                    out=acc[:],
-                    lhsT=w1_w[:, e, 2 * P * c : 2 * P * (c + 1)].bitcast(E2M1X4),
-                    lhsT_scale=w1_s[:, e, P * c : P * (c + 1)],
-                    rhs=da_w[e][:].bitcast(E5M2X4),
-                    rhs_scale=da_s[e][:],
-                    start=True,
-                    stop=True,
-                )
-                nc.scalar.copy(out=dx[e][c][:], in_=acc[:])
+        def expert(e, c):
+            acc = psum.tile([P, BANK], F32, name="acc")
+            nc.tensor.matmul_mx(
+                out=acc[:],
+                lhsT=w1_w[:, e, 2 * P * c : 2 * P * (c + 1)].bitcast(E2M1X4),
+                lhsT_scale=w1_s[:, e, P * c : P * (c + 1)],
+                rhs=da_w[e][:].bitcast(E5M2X4),
+                rhs_scale=da_s[e][:],
+                start=True,
+                stop=True,
+            )
+            return acc
 
-        def scatter(e, c):
-            nc.vector.tensor_copy(res[c][:].indirect(entries(e, 0, C)), dx[e][c][:])
+        def scatter(c, e, lo, hi, values):
+            nc.vector.tensor_copy(res[c][:].indirect(entries(e, lo, hi)), values)
+
+        def quarter(u):
+            return slice(u * QUARTER, (u + 1) * QUARTER)
+
+        def signs0(u):
+            nc.scalar.activation(woven(sign0[u]), planes(a0[u // 2][:, :, quarter(u % 2)]), ACT.Sign)
 
         for t in range(PACK):
-            gather(gated0, 0, t, 0, C)
-        for h in range(2):
-            nc.scalar.activation(woven(sign0[h]), planes(a0[h]), ACT.Sign)
-        for h in range(2):
-            nc.scalar.copy(out=woven(rounded0[h]), in_=planes(gated0[:, :, h * HALF : (h + 1) * HALF]))
-        gather(gated1, 1, 3, 0, C)
-        for h in range(2):
-            nc.vector.tensor_scalar(keep0[h], sign0[h], 0.0, None, ALU.max)
-        gather(gated1, 1, 2, 0, C)
-        for h in range(2):
-            nc.vector.tensor_tensor(da[0][:, woven_half(h)], rounded0[h], keep0[h], ALU.mult)
-        gather(gated1, 1, 1, 0, HALF)
-        quantise(0)
-        expert(0)
-        gather(gated1, 1, 1, HALF, C)
-        gather(gated1, 1, 0, 0, C)
+            nc.vector.tensor_tensor(gated0[:, t, :], dc[t][:].indirect(entries(0, 0, C)), gates[0], ALU.mult)
+        nc.vector.tensor_copy(raw1[:, 3, :], dc[3][:].indirect(entries(1, 0, C)))
 
-        nc.scalar.activation(woven(sign1), planes(a1[:]), ACT.Sign)
+        signs0(0)
+        nc.scalar.activation(keep_first, sign0[0].rearrange("p (j x) -> p j x", j=PACK), ACT.Relu)
+        nc.gpsimd.tensor_tensor(
+            da0[:, 0 : PACK * QUARTER].rearrange("p (j c t) -> p j c t", j=PACK, t=PACK),
+            gated0[:, :, quarter(0)].rearrange("p t (j c) -> p j c t", j=PACK),
+            keep_first.rearrange("p j (c t) -> p j c t", t=PACK),
+            ALU.mult,
+        )
+        quantise(0, 0, QUARTER, da0[:, 0 : PACK * QUARTER])
+        acc = psum.tile([P, BANK], F32, name="acc")
+        nc.tensor.matmul_mx(
+            out=acc[:],
+            lhsT=da_w[0][:, quarter(0)].bitcast(E5M2X4),
+            lhsT_scale=da_s[0][:, quarter(0)],
+            rhs=w1_w[:, 0, :].bitcast(E2M1X4),
+            rhs_scale=w1_s[:, 0, :],
+            start=True,
+            stop=True,
+        )
+        dx_first = []
+        for lo, hi, tag in ((0, P, "by_slot_first"), (P, K, "after_turn")):
+            by_slot = sb.tile([P, hi - lo], F32, name="by_slot%d" % lo, tag=tag, align_bytes=64)
+            nc.scalar.copy(out=by_slot[:], in_=acc[:, lo:hi])
+            turned = psum.tile([P, BANK], F32, name="acc")
+            for k0 in range(0, hi - lo, P):
+                nc.tensor.transpose(turned[:, k0 : k0 + P], by_slot[:, k0 : k0 + P], identity[:])
+            by_row = sb.tile([P, hi - lo], F32, name="by_row%d" % lo)
+            nc.scalar.copy(out=by_row[:], in_=turned[:, 0 : hi - lo])
+            dx_first.extend(by_row[:, k0 : k0 + P] for k0 in range(0, hi - lo, P))
+        for t in (2, 1, 0):
+            nc.vector.tensor_copy(raw1[:, t, :], dc[t][:].indirect(entries(1, 0, C)))
+
+        for u in range(1, 4):
+            signs0(u)
+            nc.scalar.activation(keep0[u], sign0[u], ACT.Relu)
+            nc.gpsimd.tensor_tensor(
+                da0[:, (u - 1) * PACK * QUARTER : u * PACK * QUARTER].rearrange("p (c t) -> p c t", t=PACK),
+                gated0[:, :, quarter(u)].rearrange("p t c -> p c t"),
+                keep0[u].rearrange("p (c t) -> p c t", t=PACK),
+                ALU.mult,
+            )
+        res = [sb.tile([P, T], F32, name="res%d" % c) for c in range(2)]
+        for c in range(2):
+            scatter(c, 0, 0, QUARTER, dx_first[c])
+        quantise(0, QUARTER, HALF, da0[:, 0 : PACK * QUARTER])
+        quantise(0, HALF, C, da0[:, PACK * QUARTER :])
+        res.append(sb.tile([P, T], F32, name="res2", tag="after_mask0_a", align_bytes=64))
+        res.append(sb.tile([P, T], F32, name="res3", tag="after_mask0_b", align_bytes=64))
+        for c in range(2, 4):
+            scatter(c, 0, 0, QUARTER, dx_first[c])
+        last = K // P - 1
+        banks0 = [expert(0, c) for c in range(K // P)]
+        for c in range(last):
+            dx0 = sb.tile([P, C - QUARTER], F32, name="dx0%d" % c)
+            nc.scalar.copy(out=dx0[:], in_=banks0[c][:, QUARTER:])
+            scatter(c, 0, QUARTER, C, dx0[:])
+
+        dx0 = sb.tile([P, QUARTER], F32, name="dx0_free")
+        nc.scalar.copy(out=dx0[:], in_=banks0[last][:, QUARTER:HALF])
+        scatter(last, 0, QUARTER, HALF, dx0[:])
+
+        sign1 = woven_tile("sign1", C, "after_turn")
+        gated1 = sb.tile([P, PACK, C], F32, name="gated1", tag="after_quantise0", align_bytes=64)
         for h in range(2):
+            slots = slice(h * HALF, (h + 1) * HALF)
+            nc.gpsimd.tensor_tensor(
+                gated1[:, :, slots],
+                raw1[:, :, slots],
+                gates[1][:, slots].unsqueeze(1).to_broadcast([P, PACK, HALF]),
+                ALU.mult,
+            )
+        for h in range(2):
+            slots = slice(h * HALF, (h + 1) * HALF)
+            nc.scalar.activation(woven(sign1[:, woven_half(h)]), planes(a1[:, :, slots]), ACT.Sign)
             nc.scalar.activation(keep1[h], sign1[:, woven_half(h)], ACT.Relu)
             nc.scalar.copy(out=woven(rounded1[h]), in_=planes(gated1[:, :, h * HALF : (h + 1) * HALF]))
-            nc.gpsimd.tensor_tensor(da[1][:, woven_half(h)], rounded1[h], keep1[h], ALU.mult)
-
-        last = K // P - 1
-        res = [sb.tile([P, T], F32, name="res%d" % c) for c in range(last)]
-        for c in range(last):
-            scatter(0, c)
-        quantise(1)
-        expert(1)
-        res.append(sb.tile([P, T], F32, name="res%d" % last, tag="after_mask", align_bytes=64))
-        scatter(0, last)
+            nc.gpsimd.tensor_tensor(da1[:, woven_half(h)], rounded1[h], keep1[h], ALU.mult)
+        quantise(1, 0, C, da1)
+        dx0 = sb.tile([P, HALF], F32, name="dx0%d" % last, tag="after_mask1", align_bytes=64)
+        nc.scalar.copy(out=dx0[:], in_=banks0[last][:, HALF:])
+        scatter(last, 0, HALF, C, dx0[:])
         for c in range(K // P):
-            scatter(1, c)
+            dx1 = sb.tile([P, C], F32, name="dx1%d" % c)
+            nc.scalar.copy(out=dx1[:], in_=expert(1, c)[:])
+            scatter(c, 1, 0, C, dx1[:])
             nc.sync.dma_start(out=out[c * P : (c + 1) * P, :], in_=res[c][:])

@@ -24,6 +24,7 @@ BANK = 512
 BANKS = 8
 HALF = C // 2
 QUARTER = C // 4
+EDGE = 32
 LINE = 4
 PER_COLUMN = 16
 
@@ -52,22 +53,34 @@ def tile_moe_sdb_relu_kernel(
         a0 = [sb.tile([P, PACK, HALF], F32, name="a0%d" % h) for h in range(2)]
         a1 = sb.tile([P, PACK, C], F32, name="a1")
         dc = [sb.tile([P, T], F32, name="dc%d" % t) for t in range(PACK)]
-        gated0 = sb.tile([P, PACK, C], F32, name="gated0", tag="after_mask0_a", align_bytes=64)
+        gated0 = sb.tile([P, PACK, C], F32, name="gated0", align_bytes=64)
 
-        piece = QUARTER // 2
-        reused = sb.tile([P, piece + PACK * C], F32, name="reused", align_bytes=64)
-        raw1 = reused[:, piece:].rearrange("p (t c) -> p t c", t=PACK)
-        keep_first = reused[:, 0 : PACK * C].bitcast(BF16).rearrange("p (j x) -> p j x", j=PACK)[:, :, 0:QUARTER]
+        raw1 = sb.tile([P, PACK, C], F32, name="raw1", align_bytes=64)
+        flat1 = raw1[:].rearrange("p t c -> p (t c)")
+        first_piece, second_piece = C - QUARTER // 2, 2 * C
+        piece_step = second_piece - first_piece
+        lead = QUARTER // 2
+        keep_first = (
+            flat1[:, first_piece - lead : first_piece - lead + 2 * piece_step]
+            .rearrange("p (j x) -> p j x", j=2)[:, :, lead : lead + QUARTER]
+            .bitcast(BF16)
+        )
+        sign_first = raw1[:, 2, HALF:].bitcast(BF16)
 
         def woven_tile(name, slots, tag=None):
             return sb.tile([P, slots * PACK], BF16, name=name, tag=tag or name, align_bytes=64)[:]
 
-        sign0 = [woven_tile("sign0%d" % u, QUARTER) for u in range(4)]
-        keep0 = [None] + [woven_tile("keep0%d" % u, QUARTER, "after_mask0_b" if u == 3 else None) for u in range(1, 4)]
-        da0 = woven_tile("da0", 3 * QUARTER, "after_quantise0")
-        keep1 = [woven_tile("keep1%d" % h, HALF) for h in range(2)]
-        rounded1 = [woven_tile("rounded10", HALF), woven_tile("rounded11", HALF, "after_mask1")]
-        da1 = woven_tile("da1", C)
+        parts = ((C - QUARTER, C), (QUARTER, HALF - EDGE), (HALF - EDGE, C - QUARTER))
+        sign0_rest = woven_tile("sign0_rest", C - QUARTER)
+        sign0 = [sign_first] + [sign0_rest[:, u * PACK * QUARTER : (u + 1) * PACK * QUARTER] for u in range(3)]
+        keep0 = [woven_tile("keep0%d" % n, hi - lo) for n, (lo, hi) in enumerate(parts)]
+        da0 = woven_tile("da0", C - QUARTER, "after_quantise0")
+
+        def rest(ap, lo, hi):
+            return ap[:, PACK * (lo - QUARTER) : PACK * (hi - QUARTER)]
+
+        da0_first = rest(da0, C - QUARTER, C)
+        by_slot_last = rest(da0, HALF, HALF + P // 2).bitcast(F32)
         da_w = [sb.tile([P, C], U32, name="da_w%d" % e, align_bytes=64) for e in range(E)]
         da_s = [sb.tile([P, C], U8, name="da_s%d" % e, align_bytes=64) for e in range(E)]
 
@@ -175,14 +188,15 @@ def tile_moe_sdb_relu_kernel(
         nc.vector.tensor_copy(raw1[:, 3, :], dc[3][:].indirect(entries(1, 0, C)))
 
         signs0(0)
-        nc.scalar.activation(keep_first, sign0[0].rearrange("p (j x) -> p j x", j=PACK), ACT.Relu)
+        nc.scalar.activation(keep_first, sign0[0].rearrange("p (j x) -> p j x", j=2), ACT.Relu)
         nc.gpsimd.tensor_tensor(
-            da0[:, 0 : PACK * QUARTER].rearrange("p (j c t) -> p j c t", j=PACK, t=PACK),
-            gated0[:, :, quarter(0)].rearrange("p t (j c) -> p j c t", j=PACK),
+            da0_first.rearrange("p (j c t) -> p j c t", j=2, t=PACK),
+            gated0[:, :, quarter(0)].rearrange("p t (j c) -> p j c t", j=2),
             keep_first.rearrange("p j (c t) -> p j c t", t=PACK),
             ALU.mult,
         )
-        quantise(0, 0, QUARTER, da0[:, 0 : PACK * QUARTER])
+        nc.vector.tensor_copy(raw1[:, 2, HALF:], dc[2][:].indirect(entries(1, HALF, C)))
+        quantise(0, 0, QUARTER, da0_first)
         acc = psum.tile([P, BANK], F32, name="acc")
         nc.tensor.matmul_mx(
             out=acc[:],
@@ -193,51 +207,55 @@ def tile_moe_sdb_relu_kernel(
             start=True,
             stop=True,
         )
-        dx_first = []
-        for lo, hi, tag in ((0, P, "by_slot_first"), (P, K, "after_turn")):
-            by_slot = sb.tile([P, hi - lo], F32, name="by_slot%d" % lo, tag=tag, align_bytes=64)
-            nc.scalar.copy(out=by_slot[:], in_=acc[:, lo:hi])
-            turned = psum.tile([P, BANK], F32, name="acc")
-            for k0 in range(0, hi - lo, P):
-                nc.tensor.transpose(turned[:, k0 : k0 + P], by_slot[:, k0 : k0 + P], identity[:])
-            by_row = sb.tile([P, hi - lo], F32, name="by_row%d" % lo)
-            nc.scalar.copy(out=by_row[:], in_=turned[:, 0 : hi - lo])
-            dx_first.extend(by_row[:, k0 : k0 + P] for k0 in range(0, hi - lo, P))
-        for t in (2, 1, 0):
+        by_slot_first = sb.tile([P, P], F32, name="by_slot_first")
+        nc.scalar.copy(out=by_slot_first[:], in_=acc[:, 0:P])
+        turned = psum.tile([P, BANK], F32, name="acc")
+        nc.tensor.transpose(turned[:, 0:P], by_slot_first[:], identity[:])
+        by_row_first = sb.tile([P, P], F32, name="by_row_first")
+        nc.scalar.copy(out=by_row_first[:], in_=turned[:, 0:P])
+        by_slot_middle = sb.tile([P, 2 * P], F32, name="by_slot_middle")
+        nc.scalar.copy(out=by_slot_middle[:], in_=acc[:, P : 3 * P])
+        nc.scalar.copy(out=by_slot_last, in_=acc[:, 3 * P :])
+        turned = psum.tile([P, BANK], F32, name="acc")
+        for j, by_slot in enumerate((by_slot_middle[:, 0:P], by_slot_middle[:, P:], by_slot_last)):
+            nc.tensor.transpose(turned[:, j * P : (j + 1) * P], by_slot, identity[:])
+        by_row_rest = sb.tile([P, K - P], F32, name="by_row_rest")
+        nc.scalar.copy(out=by_row_rest[:], in_=turned[:, 0 : K - P])
+        dx_first = [by_row_first[:]] + [by_row_rest[:, j * P : (j + 1) * P] for j in range(3)]
+        nc.vector.tensor_copy(raw1[:, 2, 0:HALF], dc[2][:].indirect(entries(1, 0, HALF)))
+        for t in (1, 0):
             nc.vector.tensor_copy(raw1[:, t, :], dc[t][:].indirect(entries(1, 0, C)))
 
-        for u in range(1, 4):
+        for u, keep, (lo, hi) in zip((3, 1, 2), keep0, parts):
             signs0(u)
-            nc.scalar.activation(keep0[u], sign0[u], ACT.Relu)
+            nc.scalar.activation(keep, rest(sign0_rest, lo, hi), ACT.Relu)
             nc.gpsimd.tensor_tensor(
-                da0[:, (u - 1) * PACK * QUARTER : u * PACK * QUARTER].rearrange("p (c t) -> p c t", t=PACK),
-                gated0[:, :, quarter(u)].rearrange("p t c -> p c t"),
-                keep0[u].rearrange("p (c t) -> p c t", t=PACK),
+                rest(da0, lo, hi).rearrange("p (c t) -> p c t", t=PACK),
+                gated0[:, :, lo:hi].rearrange("p t c -> p c t"),
+                keep.rearrange("p (c t) -> p c t", t=PACK),
                 ALU.mult,
             )
+        last = K // P - 1
         res = [sb.tile([P, T], F32, name="res%d" % c) for c in range(2)]
         for c in range(2):
             scatter(c, 0, 0, QUARTER, dx_first[c])
-        quantise(0, QUARTER, HALF, da0[:, 0 : PACK * QUARTER])
-        quantise(0, HALF, C, da0[:, PACK * QUARTER :])
-        res.append(sb.tile([P, T], F32, name="res2", tag="after_mask0_a", align_bytes=64))
-        res.append(sb.tile([P, T], F32, name="res3", tag="after_mask0_b", align_bytes=64))
-        for c in range(2, 4):
+        quantise(0, QUARTER, HALF, rest(da0, QUARTER, HALF))
+        quantise(0, HALF, C, rest(da0, HALF, C))
+        for c, tag in ((2, "gated0"), (3, "keep02")):
+            res.append(sb.tile([P, T], F32, name="res%d" % c, tag=tag, align_bytes=64))
             scatter(c, 0, 0, QUARTER, dx_first[c])
-        last = K // P - 1
         banks0 = [expert(0, c) for c in range(K // P)]
         for c in range(last):
             dx0 = sb.tile([P, C - QUARTER], F32, name="dx0%d" % c)
             nc.scalar.copy(out=dx0[:], in_=banks0[c][:, QUARTER:])
             scatter(c, 0, QUARTER, C, dx0[:])
-
         dx0 = sb.tile([P, QUARTER], F32, name="dx0_free")
         nc.scalar.copy(out=dx0[:], in_=banks0[last][:, QUARTER:HALF])
         scatter(last, 0, QUARTER, HALF, dx0[:])
 
-        sign1 = woven_tile("sign1", C, "after_turn")
+        sign1 = [woven_tile("sign10", HALF, "da_s0"), woven_tile("sign11", HALF, "keep01")]
         gated1 = sb.tile([P, PACK, C], F32, name="gated1", tag="after_quantise0", align_bytes=64)
-        for h in range(2):
+        for h in (1, 0):
             slots = slice(h * HALF, (h + 1) * HALF)
             nc.gpsimd.tensor_tensor(
                 gated1[:, :, slots],
@@ -245,14 +263,16 @@ def tile_moe_sdb_relu_kernel(
                 gates[1][:, slots].unsqueeze(1).to_broadcast([P, PACK, HALF]),
                 ALU.mult,
             )
-        for h in range(2):
-            slots = slice(h * HALF, (h + 1) * HALF)
-            nc.scalar.activation(woven(sign1[:, woven_half(h)]), planes(a1[:, :, slots]), ACT.Sign)
-            nc.scalar.activation(keep1[h], sign1[:, woven_half(h)], ACT.Relu)
-            nc.scalar.copy(out=woven(rounded1[h]), in_=planes(gated1[:, :, h * HALF : (h + 1) * HALF]))
-            nc.gpsimd.tensor_tensor(da1[:, woven_half(h)], rounded1[h], keep1[h], ALU.mult)
+        da1 = woven_tile("da1", C)
+        for h in (1, 0):
+            keep1 = woven_tile("keep1%d" % h, HALF)
+            rounded1 = woven_tile("rounded1%d" % h, HALF)
+            nc.scalar.activation(woven(sign1[h]), planes(a1[:, :, h * HALF : (h + 1) * HALF]), ACT.Sign)
+            nc.scalar.activation(keep1, sign1[h], ACT.Relu)
+            nc.scalar.copy(out=woven(rounded1), in_=planes(gated1[:, :, h * HALF : (h + 1) * HALF]))
+            nc.gpsimd.tensor_tensor(da1[:, woven_half(h)], rounded1, keep1, ALU.mult)
         quantise(1, 0, C, da1)
-        dx0 = sb.tile([P, HALF], F32, name="dx0%d" % last, tag="after_mask1", align_bytes=64)
+        dx0 = sb.tile([P, HALF], F32, name="dx0%d" % last, tag="rounded10", align_bytes=64)
         nc.scalar.copy(out=dx0[:], in_=banks0[last][:, HALF:])
         scatter(last, 0, HALF, C, dx0[:])
         for c in range(K // P):

@@ -90,25 +90,26 @@ def tile_moe_sdb_relu_kernel(
         def scale_rows(q):
             return slice(4 * q, 4 * q + 4)
 
-        def load_dy_scales(q):
-            nc.sync.dma_start(
+        def load_dy_scales(q, queue):
+            queue.dma_start(
                 out=dy_s[scale_partitions(q), :].bitcast(I32), in_=dy_scales[0, scale_rows(q), :].bitcast(I32)
             )
 
-        nc.vector.memset(w2_raw_s[:].bitcast(U32), 0)
-        for q in range(QUADS // 2):
-            load_dy_scales(q)
+        w2_rows = w2t_scales[0].bitcast(I32)
+        load_dy_scales(0, nc.sync)
+        load_dy_scales(1, nc.scalar)
+        nc.sync.dma_start(out=w2_raw_s[0:16, :].bitcast(I32), in_=w2_rows)
+        nc.scalar.dma_start(out=w2_raw_s[16:128, :].bitcast(I32), in_=w2_rows[2:16, :].partition_broadcast(8))
         nc.sync.dma_start(out=w2_raw_w[:].bitcast(I32), in_=w2t_words[0].bitcast(I32))
-        nc.sync.dma_start(out=dy_w[:].bitcast(I32), in_=dy_words[0].rearrange("p t d -> p (t d)").bitcast(I32))
-        for q in range(QUADS):
-            nc.sync.dma_start(
-                out=w2_raw_s[scale_partitions(q), :].bitcast(I32), in_=w2t_scales[0, scale_rows(q), :].bitcast(I32)
-            )
-        for q in range(QUADS // 2, QUADS):
-            load_dy_scales(q)
+        for q in range(2, QUADS):
+            load_dy_scales(q, nc.scalar)
+        dy_rows = dy_words[0].rearrange("p t d -> p (t d)").bitcast(I32)
+        for b in range(T // BANK):
+            tokens = slice(b * BANK, (b + 1) * BANK)
+            nc.sync.dma_start(out=dy_w[:, tokens].bitcast(I32), in_=dy_rows[:, tokens])
         a_planes = a.rearrange("(p t) j -> p t j", t=PACK)
-        nc.sync.dma_start(out=gates[0], in_=gate[:, 0:C])
         nc.sync.dma_start(offsets[:], offs)
+        nc.sync.dma_start(out=gates[0], in_=gate[:, 0:C])
         for h in range(2):
             nc.sync.dma_start(out=a0[h][:], in_=a_planes[:, :, h * HALF : (h + 1) * HALF])
         nc.sync.dma_start(out=gates[1], in_=gate[:, C : 2 * C])

@@ -35,7 +35,10 @@ def tile_moe_sdb_relu_kernel(
     nc = tc.nc
     with ExitStack() as ctx:
         sb = ctx.enter_context(tc.tile_pool(name="sb", bufs=1))
-        psum = ctx.enter_context(tc.psum_pool(name="psum", bufs=BANKS))
+        psum = ctx.enter_context(tc.psum_pool(name="psum", bufs=1))
+
+        def bank_tile(name, first, count=1):
+            return psum.tile([P, count * BANK], F32, name=name, offset=first * BANK * 4)
 
         offsets = sb.tile([P, E * C // PER_COLUMN], U16, name="offsets")
         dy_w = sb.tile([P, T], U32, name="dy_w", align_bytes=64)
@@ -46,7 +49,9 @@ def tile_moe_sdb_relu_kernel(
         w2_s = sb.tile([P, H], U8, name="w2_s", align_bytes=64)
         w1_w = sb.tile([P, E, 2 * K], U8, name="w1_w", align_bytes=64)
         w1_s = sb.tile([P, E, K], U8, name="w1_s", align_bytes=64)
-        gates = [sb.tile([P, C], F32, name="gate%d" % e)[:] for e in range(E)]
+        gate0 = sb.tile([P, C], F32, name="gate0")[:]
+        gate1_rows = sb.tile([P, HALF], F32, name="gate1_rows")[:]
+        gate1_columns = sb.tile([P, 2], F32, name="gate1_columns")[:]
 
         identity = sb.tile([P, P], F32, name="identity")
         make_identity(nc, identity[:])
@@ -109,10 +114,10 @@ def tile_moe_sdb_relu_kernel(
             nc.sync.dma_start(out=dy_w[:, tokens].bitcast(I32), in_=dy_rows[:, tokens])
         a_planes = a.rearrange("(p t) j -> p t j", t=PACK)
         nc.sync.dma_start(offsets[:], offs)
-        nc.sync.dma_start(out=gates[0], in_=gate[:, 0:C])
+        nc.sync.dma_start(out=gate0, in_=gate[:, 0:C])
         for h in range(2):
             nc.sync.dma_start(out=a0[h][:], in_=a_planes[:, :, h * HALF : (h + 1) * HALF])
-        nc.sync.dma_start(out=gates[1], in_=gate[:, C : 2 * C])
+        nc.sync.dma_start(out=gate1_rows, in_=gate[:, C + HALF : 2 * C])
         nc.sync.dma_start(out=w1_w[:].bitcast(I32), in_=w1t_words[:, 0].rearrange("e p b -> p e b").bitcast(I32))
         for q in range(QUADS):
             nc.sync.dma_start(
@@ -120,6 +125,8 @@ def tile_moe_sdb_relu_kernel(
                 in_=w1t_scales[:, 0, scale_rows(q), :].rearrange("e r k -> r e k").bitcast(I32),
             )
         nc.sync.dma_start(out=a1[:], in_=a_planes[:, :, C : 2 * C])
+        with nc.allow_non_contiguous_dma(reason="256 gates, one slot on each partition"):
+            nc.sync.dma_start(out=gate1_columns, in_=gate[0, C : C + HALF].rearrange("(q p) -> p q", p=P))
 
         w_src = w2_raw_w[:].bitcast(U16).rearrange("p (m t) -> p t m", t=PACK)
         w_dst = w2_w[:].bitcast(U16).rearrange("p (t m) -> p t m", t=PACK)
@@ -130,9 +137,9 @@ def tile_moe_sdb_relu_kernel(
             nc.vector.tensor_copy(out=s_dst[:, some_planes, :], in_=s_src[:, some_planes, :])
 
         for t in range(PACK):
-            for b in range(T // BANK):
+            for b in (0, 1) if t == 0 else (1, 0):
                 tokens = slice(b * BANK, (b + 1) * BANK)
-                acc = psum.tile([P, BANK], F32, name="acc")
+                acc = bank_tile("dc_acc%d%d" % (t, b), t + 1 if b else max(t - 1, 0))
                 nc.tensor.matmul_mx(
                     out=acc[:],
                     lhsT=w2_w[:, 2 * P * t : 2 * P * (t + 1)].bitcast(E2M1X4),
@@ -163,7 +170,7 @@ def tile_moe_sdb_relu_kernel(
             nc.vector.quantize_mx(out=da_w[e][:, lo:hi].bitcast(E5M2X4), scales=da_s[e][:, lo:hi], in_=values)
 
         def expert(e, c):
-            acc = psum.tile([P, BANK], F32, name="acc")
+            acc = bank_tile("dx_acc%d%d" % (e, c), c + PACK * (1 - e))
             nc.tensor.matmul_mx(
                 out=acc[:],
                 lhsT=w1_w[:, e, 2 * P * c : 2 * P * (c + 1)].bitcast(E2M1X4),
@@ -185,7 +192,7 @@ def tile_moe_sdb_relu_kernel(
             nc.scalar.activation(woven(sign0[u]), planes(a0[u // 2][:, :, quarter(u % 2)]), ACT.Sign)
 
         for t in range(PACK):
-            nc.vector.tensor_tensor(gated0[:, t, :], dc[t][:].indirect(entries(0, 0, C)), gates[0], ALU.mult)
+            nc.vector.tensor_tensor(gated0[:, t, :], dc[t][:].indirect(entries(0, 0, C)), gate0, ALU.mult)
         nc.vector.tensor_copy(raw1[:, 3, :], dc[3][:].indirect(entries(1, 0, C)))
 
         signs0(0)
@@ -198,7 +205,7 @@ def tile_moe_sdb_relu_kernel(
         )
         nc.vector.tensor_copy(raw1[:, 2, HALF:], dc[2][:].indirect(entries(1, HALF, C)))
         quantise(0, 0, QUARTER, da0_first)
-        acc = psum.tile([P, BANK], F32, name="acc")
+        acc = bank_tile("early_acc", 0)
         nc.tensor.matmul_mx(
             out=acc[:],
             lhsT=da_w[0][:, quarter(0)].bitcast(E5M2X4),
@@ -210,14 +217,14 @@ def tile_moe_sdb_relu_kernel(
         )
         by_slot_first = sb.tile([P, P], F32, name="by_slot_first")
         nc.scalar.copy(out=by_slot_first[:], in_=acc[:, 0:P])
-        turned = psum.tile([P, BANK], F32, name="acc")
+        turned = bank_tile("turned_first", 1)
         nc.tensor.transpose(turned[:, 0:P], by_slot_first[:], identity[:])
         by_row_first = sb.tile([P, P], F32, name="by_row_first")
         nc.scalar.copy(out=by_row_first[:], in_=turned[:, 0:P])
         by_slot_middle = sb.tile([P, 2 * P], F32, name="by_slot_middle")
         nc.scalar.copy(out=by_slot_middle[:], in_=acc[:, P : 3 * P])
         nc.scalar.copy(out=by_slot_last, in_=acc[:, 3 * P :])
-        turned = psum.tile([P, BANK], F32, name="acc")
+        turned = bank_tile("turned_rest", 2)
         for j, by_slot in enumerate((by_slot_middle[:, 0:P], by_slot_middle[:, P:], by_slot_last)):
             nc.tensor.transpose(turned[:, j * P : (j + 1) * P], by_slot, identity[:])
         by_row_rest = sb.tile([P, K - P], F32, name="by_row_rest")
@@ -245,37 +252,62 @@ def tile_moe_sdb_relu_kernel(
         for c, tag in ((2, "gated0"), (3, "keep02")):
             res.append(sb.tile([P, T], F32, name="res%d" % c, tag=tag, align_bytes=64))
             scatter(c, 0, 0, QUARTER, dx_first[c])
+        raw_by_slot = bank_tile("raw_by_slot", 2, 2)
+        for u in range(2):
+            for t in range(PACK):
+                column = u * BANK + t * P
+                nc.tensor.transpose(raw_by_slot[:, column : column + P], raw1[:, t, quarter(u)], identity[:])
         banks0 = [expert(0, c) for c in range(K // P)]
         for c in range(last):
             dx0 = sb.tile([P, C - QUARTER], F32, name="dx0%d" % c)
             nc.scalar.copy(out=dx0[:], in_=banks0[c][:, QUARTER:])
             scatter(c, 0, QUARTER, C, dx0[:])
-        dx0 = sb.tile([P, QUARTER], F32, name="dx0_free")
-        nc.scalar.copy(out=dx0[:], in_=banks0[last][:, QUARTER:HALF])
-        scatter(last, 0, QUARTER, HALF, dx0[:])
 
         sign1 = [woven_tile("sign10", HALF, "da_s0"), woven_tile("sign11", HALF, "keep01")]
-        gated1 = sb.tile([P, PACK, C], F32, name="gated1", tag="after_quantise0", align_bytes=64)
-        for h in (1, 0):
-            slots = slice(h * HALF, (h + 1) * HALF)
-            nc.gpsimd.tensor_tensor(
-                gated1[:, :, slots],
-                raw1[:, :, slots],
-                gates[1][:, slots].unsqueeze(1).to_broadcast([P, PACK, HALF]),
-                ALU.mult,
-            )
+        keep1 = [woven_tile("keep1%d" % h, HALF) for h in range(2)]
+        gated1 = sb.tile([P, PACK, HALF], F32, name="gated1", tag="after_quantise0", align_bytes=64)
         da1 = woven_tile("da1", C)
-        for h in (1, 0):
-            keep1 = woven_tile("keep1%d" % h, HALF)
-            rounded1 = woven_tile("rounded1%d" % h, HALF)
+
+        def masks1(h):
             nc.scalar.activation(woven(sign1[h]), planes(a1[:, :, h * HALF : (h + 1) * HALF]), ACT.Sign)
-            nc.scalar.activation(keep1, sign1[h], ACT.Relu)
-            nc.scalar.copy(out=woven(rounded1), in_=planes(gated1[:, :, h * HALF : (h + 1) * HALF]))
-            nc.gpsimd.tensor_tensor(da1[:, woven_half(h)], rounded1, keep1, ALU.mult)
+            nc.scalar.activation(keep1[h], sign1[h], ACT.Relu)
+
+        nc.gpsimd.tensor_tensor(
+            gated1[:], raw1[:, :, HALF:], gate1_rows.unsqueeze(1).to_broadcast([P, PACK, HALF]), ALU.mult
+        )
+        masks1(1)
+        nc.gpsimd.tensor_tensor(
+            da1[:, woven_half(1)].rearrange("p (c t) -> p c t", t=PACK),
+            gated1[:].rearrange("p t c -> p c t"),
+            keep1[1].rearrange("p (c t) -> p c t", t=PACK),
+            ALU.mult,
+        )
+        both_pairs = woven_tile("both_pairs", HALF, "sign0_rest")
+        pairs_by_row = bank_tile("pairs_by_row", PACK)
+        for u in range(2):
+            pairs = both_pairs[:, u * PACK * QUARTER : (u + 1) * PACK * QUARTER]
+            nc.scalar.activation(
+                pairs.rearrange("s (w p e) -> s w p e", w=2, e=2),
+                raw_by_slot[:, u * BANK : (u + 1) * BANK].rearrange("s (w e p) -> s w p e", w=2, e=2),
+                ACT.Copy,
+                scale=gate1_columns[:, u : u + 1],
+            )
+            for w in range(2):
+                column = (2 * u + w) * P
+                nc.tensor.transpose(
+                    pairs_by_row[:, column : column + P], pairs.bitcast(F32)[:, w * P : (w + 1) * P], identity[:]
+                )
+        rounded1 = woven_tile("rounded1", HALF)
+        nc.scalar.copy(
+            out=rounded1.bitcast(F32).rearrange("p (u s w) -> p u s w", u=2, w=2),
+            in_=pairs_by_row[:].rearrange("p (u w s) -> p u s w", u=2, w=2),
+        )
+        masks1(0)
+        nc.gpsimd.tensor_tensor(da1[:, woven_half(0)], rounded1, keep1[0], ALU.mult)
         quantise(1, 0, C, da1)
-        dx0 = sb.tile([P, HALF], F32, name="dx0%d" % last, tag="rounded10", align_bytes=64)
-        nc.scalar.copy(out=dx0[:], in_=banks0[last][:, HALF:])
-        scatter(last, 0, HALF, C, dx0[:])
+        dx0 = sb.tile([P, C - QUARTER], F32, name="dx0%d" % last, tag="keep10", align_bytes=64)
+        nc.scalar.copy(out=dx0[:], in_=banks0[last][:, QUARTER:])
+        scatter(last, 0, QUARTER, C, dx0[:])
         for c in range(K // P):
             dx1 = sb.tile([P, C], F32, name="dx1%d" % c)
             nc.scalar.copy(out=dx1[:], in_=expert(1, c)[:])

@@ -58,18 +58,13 @@ def tile_moe_sdb_relu_kernel(
         a0 = [sb.tile([P, PACK, HALF], F32, name="a0%d" % h) for h in range(2)]
         a1 = sb.tile([P, PACK, C], F32, name="a1")
         dc = [sb.tile([P, T], F32, name="dc%d" % t) for t in range(PACK)]
-        gated0 = sb.tile([P, PACK, C], F32, name="gated0", align_bytes=64)
+        gated0_all = sb.tile([P, PACK * (C + QUARTER)], F32, name="gated0", align_bytes=64)
+        gated0 = gated0_all[:].rearrange("p (t c) -> p t c", t=PACK)[:, :, QUARTER:]
+        held_half = gated0_all[:, 3 * (C + QUARTER) : 3 * (C + QUARTER) + HALF]
 
         raw1 = sb.tile([P, PACK, C], F32, name="raw1", align_bytes=64)
         flat1 = raw1[:].rearrange("p t c -> p (t c)")
-        first_piece, second_piece = C - QUARTER // 2, 2 * C
-        piece_step = second_piece - first_piece
-        lead = QUARTER // 2
-        keep_first = (
-            flat1[:, first_piece - lead : first_piece - lead + 2 * piece_step]
-            .rearrange("p (j x) -> p j x", j=2)[:, :, lead : lead + QUARTER]
-            .bitcast(BF16)
-        )
+        keep_first = flat1[:, C - QUARTER : C + QUARTER].bitcast(BF16)
         sign_first = raw1[:, 2, HALF:].bitcast(BF16)
 
         def woven_tile(name, slots, tag=None):
@@ -163,6 +158,9 @@ def tile_moe_sdb_relu_kernel(
         def planes(ap):
             return ap.rearrange("p t (c i) -> p c t i", i=LINE)
 
+        def by_lines(ap):
+            return ap.rearrange("p (c t i) -> p c t i", i=LINE, t=PACK)
+
         def woven_half(h):
             return slice(h * HALF * PACK, (h + 1) * HALF * PACK)
 
@@ -189,20 +187,15 @@ def tile_moe_sdb_relu_kernel(
             return slice(u * QUARTER, (u + 1) * QUARTER)
 
         def signs0(u):
-            nc.scalar.activation(woven(sign0[u]), planes(a0[u // 2][:, :, quarter(u % 2)]), ACT.Sign)
+            nc.scalar.activation(by_lines(sign0[u]), planes(a0[u // 2][:, :, quarter(u % 2)]), ACT.Sign)
 
         for t in range(PACK):
             nc.vector.tensor_tensor(gated0[:, t, :], dc[t][:].indirect(entries(0, 0, C)), gate0, ALU.mult)
         nc.vector.tensor_copy(raw1[:, 3, :], dc[3][:].indirect(entries(1, 0, C)))
 
         signs0(0)
-        nc.scalar.activation(keep_first, sign0[0].rearrange("p (j x) -> p j x", j=2), ACT.Relu)
-        nc.gpsimd.tensor_tensor(
-            da0_first.rearrange("p (j c t) -> p j c t", j=2, t=PACK),
-            gated0[:, :, quarter(0)].rearrange("p t (j c) -> p j c t", j=2),
-            keep_first.rearrange("p j (c t) -> p j c t", t=PACK),
-            ALU.mult,
-        )
+        nc.scalar.activation(keep_first, sign0[0], ACT.Relu)
+        nc.gpsimd.tensor_tensor(woven(da0_first), planes(gated0[:, :, quarter(0)]), by_lines(keep_first), ALU.mult)
         nc.vector.tensor_copy(raw1[:, 2, HALF:], dc[2][:].indirect(entries(1, HALF, C)))
         quantise(0, 0, QUARTER, da0_first)
         acc = bank_tile("early_acc", 0)
@@ -230,19 +223,14 @@ def tile_moe_sdb_relu_kernel(
         by_row_rest = sb.tile([P, K - P], F32, name="by_row_rest")
         nc.scalar.copy(out=by_row_rest[:], in_=turned[:, 0 : K - P])
         dx_first = [by_row_first[:]] + [by_row_rest[:, j * P : (j + 1) * P] for j in range(3)]
-        nc.vector.tensor_copy(raw1[:, 2, 0:HALF], dc[2][:].indirect(entries(1, 0, HALF)))
+        nc.vector.tensor_copy(held_half, dc[2][:].indirect(entries(1, 0, HALF)))
         for t in (1, 0):
             nc.vector.tensor_copy(raw1[:, t, :], dc[t][:].indirect(entries(1, 0, C)))
 
         for u, keep, (lo, hi) in zip((3, 1, 2), keep0, parts):
             signs0(u)
             nc.scalar.activation(keep, rest(sign0_rest, lo, hi), ACT.Relu)
-            nc.gpsimd.tensor_tensor(
-                rest(da0, lo, hi).rearrange("p (c t) -> p c t", t=PACK),
-                gated0[:, :, lo:hi].rearrange("p t c -> p c t"),
-                keep.rearrange("p (c t) -> p c t", t=PACK),
-                ALU.mult,
-            )
+            nc.gpsimd.tensor_tensor(woven(rest(da0, lo, hi)), planes(gated0[:, :, lo:hi]), by_lines(keep), ALU.mult)
         last = K // P - 1
         res = [sb.tile([P, T], F32, name="res%d" % c) for c in range(2)]
         for c in range(2):
@@ -256,9 +244,10 @@ def tile_moe_sdb_relu_kernel(
         for u in range(2):
             for t in range(PACK):
                 column = u * BANK + t * P
-                nc.tensor.transpose(raw_by_slot[:, column : column + P], raw1[:, t, quarter(u)], identity[:])
+                rows = held_half[:, quarter(u)] if t == 2 else raw1[:, t, quarter(u)]
+                nc.tensor.transpose(raw_by_slot[:, column : column + P], rows, identity[:])
         banks0 = [expert(0, c) for c in range(K // P)]
-        for c in range(last):
+        for c in range(last - 1):
             dx0 = sb.tile([P, C - QUARTER], F32, name="dx0%d" % c)
             nc.scalar.copy(out=dx0[:], in_=banks0[c][:, QUARTER:])
             scatter(c, 0, QUARTER, C, dx0[:])
@@ -269,20 +258,15 @@ def tile_moe_sdb_relu_kernel(
         da1 = woven_tile("da1", C)
 
         def masks1(h):
-            nc.scalar.activation(woven(sign1[h]), planes(a1[:, :, h * HALF : (h + 1) * HALF]), ACT.Sign)
+            nc.scalar.activation((woven, by_lines)[h](sign1[h]), planes(a1[:, :, h * HALF : (h + 1) * HALF]), ACT.Sign)
             nc.scalar.activation(keep1[h], sign1[h], ACT.Relu)
 
         nc.gpsimd.tensor_tensor(
             gated1[:], raw1[:, :, HALF:], gate1_rows.unsqueeze(1).to_broadcast([P, PACK, HALF]), ALU.mult
         )
         masks1(1)
-        nc.gpsimd.tensor_tensor(
-            da1[:, woven_half(1)].rearrange("p (c t) -> p c t", t=PACK),
-            gated1[:].rearrange("p t c -> p c t"),
-            keep1[1].rearrange("p (c t) -> p c t", t=PACK),
-            ALU.mult,
-        )
-        both_pairs = woven_tile("both_pairs", HALF, "sign0_rest")
+        nc.gpsimd.tensor_tensor(woven(da1[:, woven_half(1)]), planes(gated1[:]), by_lines(keep1[1]), ALU.mult)
+        both_pairs = woven_tile("both_pairs", HALF, "da_w0")
         pairs_by_row = bank_tile("pairs_by_row", PACK)
         for u in range(2):
             pairs = both_pairs[:, u * PACK * QUARTER : (u + 1) * PACK * QUARTER]
@@ -302,12 +286,18 @@ def tile_moe_sdb_relu_kernel(
             out=rounded1.bitcast(F32).rearrange("p (u s w) -> p u s w", u=2, w=2),
             in_=pairs_by_row[:].rearrange("p (u w s) -> p u s w", u=2, w=2),
         )
+        dx0 = sb.tile([P, C - QUARTER], F32, name="dx02", tag="da_w0", align_bytes=64)
+        nc.scalar.copy(out=dx0[:], in_=banks0[last - 1][:, QUARTER:])
+        scatter(last - 1, 0, QUARTER, C, dx0[:])
         masks1(0)
+        dx0 = sb.tile([P, QUARTER], F32, name="dx0_free", tag="da_s0", align_bytes=64)
+        nc.scalar.copy(out=dx0[:], in_=banks0[last][:, QUARTER:HALF])
+        scatter(last, 0, QUARTER, HALF, dx0[:])
         nc.gpsimd.tensor_tensor(da1[:, woven_half(0)], rounded1, keep1[0], ALU.mult)
         quantise(1, 0, C, da1)
-        dx0 = sb.tile([P, C - QUARTER], F32, name="dx0%d" % last, tag="keep10", align_bytes=64)
-        nc.scalar.copy(out=dx0[:], in_=banks0[last][:, QUARTER:])
-        scatter(last, 0, QUARTER, C, dx0[:])
+        dx0 = sb.tile([P, HALF], F32, name="dx0%d" % last, tag="keep10", align_bytes=64)
+        nc.scalar.copy(out=dx0[:], in_=banks0[last][:, HALF:])
+        scatter(last, 0, HALF, C, dx0[:])
         for c in range(K // P):
             dx1 = sb.tile([P, C], F32, name="dx1%d" % c)
             nc.scalar.copy(out=dx1[:], in_=expert(1, c)[:])

@@ -58,13 +58,11 @@ def tile_moe_sdb_relu_kernel(
         a0 = [sb.tile([P, PACK, HALF], F32, name="a0%d" % h) for h in range(2)]
         a1 = sb.tile([P, PACK, C], F32, name="a1")
         dc = [sb.tile([P, T], F32, name="dc%d" % t) for t in range(PACK)]
-        gated0_all = sb.tile([P, PACK * (C + QUARTER)], F32, name="gated0", align_bytes=64)
-        gated0 = gated0_all[:].rearrange("p (t c) -> p t c", t=PACK)[:, :, QUARTER:]
-        held_half = gated0_all[:, 3 * (C + QUARTER) : 3 * (C + QUARTER) + HALF]
+        gated0 = sb.tile([P, PACK, C], F32, name="gated0", align_bytes=64)
 
         raw1 = sb.tile([P, PACK, C], F32, name="raw1", align_bytes=64)
         flat1 = raw1[:].rearrange("p t c -> p (t c)")
-        keep_first = flat1[:, C - QUARTER : C + QUARTER].bitcast(BF16)
+        keep_first = flat1[:, 2 * C - QUARTER : 2 * C + QUARTER].bitcast(BF16)
         sign_first = raw1[:, 2, HALF:].bitcast(BF16)
 
         def woven_tile(name, slots, tag=None):
@@ -73,7 +71,8 @@ def tile_moe_sdb_relu_kernel(
         parts = ((C - QUARTER, C), (QUARTER, HALF - EDGE), (HALF - EDGE, C - QUARTER))
         sign0_rest = woven_tile("sign0_rest", C - QUARTER)
         sign0 = [sign_first] + [sign0_rest[:, u * PACK * QUARTER : (u + 1) * PACK * QUARTER] for u in range(3)]
-        keep0 = [woven_tile("keep0%d" % n, hi - lo) for n, (lo, hi) in enumerate(parts)]
+        keep0 = [raw1[:, 0, 0:HALF].bitcast(BF16)]
+        keep0.extend(woven_tile("keep0%d" % n, parts[n][1] - parts[n][0]) for n in (1, 2))
         da0 = woven_tile("da0", C - QUARTER, "after_quantise0")
 
         def rest(ap, lo, hi):
@@ -104,8 +103,7 @@ def tile_moe_sdb_relu_kernel(
         for q in range(2, QUADS):
             load_dy_scales(q, nc.scalar)
         dy_rows = dy_words[0].rearrange("p t d -> p (t d)").bitcast(I32)
-        for b in range(T // BANK):
-            tokens = slice(b * BANK, (b + 1) * BANK)
+        for tokens in (slice(0, BANK + QUARTER), slice(BANK + QUARTER, T)):
             nc.sync.dma_start(out=dy_w[:, tokens].bitcast(I32), in_=dy_rows[:, tokens])
         a_planes = a.rearrange("(p t) j -> p t j", t=PACK)
         nc.sync.dma_start(offsets[:], offs)
@@ -223,14 +221,14 @@ def tile_moe_sdb_relu_kernel(
         by_row_rest = sb.tile([P, K - P], F32, name="by_row_rest")
         nc.scalar.copy(out=by_row_rest[:], in_=turned[:, 0 : K - P])
         dx_first = [by_row_first[:]] + [by_row_rest[:, j * P : (j + 1) * P] for j in range(3)]
-        nc.vector.tensor_copy(held_half, dc[2][:].indirect(entries(1, 0, HALF)))
-        for t in (1, 0):
-            nc.vector.tensor_copy(raw1[:, t, :], dc[t][:].indirect(entries(1, 0, C)))
+        nc.vector.tensor_copy(raw1[:, 2, 0:HALF], dc[2][:].indirect(entries(1, 0, HALF)))
+        nc.vector.tensor_copy(raw1[:, 1, :], dc[1][:].indirect(entries(1, 0, C)))
 
         for u, keep, (lo, hi) in zip((3, 1, 2), keep0, parts):
             signs0(u)
             nc.scalar.activation(keep, rest(sign0_rest, lo, hi), ACT.Relu)
             nc.gpsimd.tensor_tensor(woven(rest(da0, lo, hi)), planes(gated0[:, :, lo:hi]), by_lines(keep), ALU.mult)
+        nc.vector.tensor_copy(raw1[:, 0, :], dc[0][:].indirect(entries(1, 0, C)))
         last = K // P - 1
         res = [sb.tile([P, T], F32, name="res%d" % c) for c in range(2)]
         for c in range(2):
@@ -244,8 +242,7 @@ def tile_moe_sdb_relu_kernel(
         for u in range(2):
             for t in range(PACK):
                 column = u * BANK + t * P
-                rows = held_half[:, quarter(u)] if t == 2 else raw1[:, t, quarter(u)]
-                nc.tensor.transpose(raw_by_slot[:, column : column + P], rows, identity[:])
+                nc.tensor.transpose(raw_by_slot[:, column : column + P], raw1[:, t, quarter(u)], identity[:])
         banks0 = [expert(0, c) for c in range(K // P)]
         for c in range(last - 1):
             dx0 = sb.tile([P, C - QUARTER], F32, name="dx0%d" % c)
@@ -290,14 +287,11 @@ def tile_moe_sdb_relu_kernel(
         nc.scalar.copy(out=dx0[:], in_=banks0[last - 1][:, QUARTER:])
         scatter(last - 1, 0, QUARTER, C, dx0[:])
         masks1(0)
-        dx0 = sb.tile([P, QUARTER], F32, name="dx0_free", tag="da_s0", align_bytes=64)
-        nc.scalar.copy(out=dx0[:], in_=banks0[last][:, QUARTER:HALF])
-        scatter(last, 0, QUARTER, HALF, dx0[:])
         nc.gpsimd.tensor_tensor(da1[:, woven_half(0)], rounded1, keep1[0], ALU.mult)
         quantise(1, 0, C, da1)
-        dx0 = sb.tile([P, HALF], F32, name="dx0%d" % last, tag="keep10", align_bytes=64)
-        nc.scalar.copy(out=dx0[:], in_=banks0[last][:, HALF:])
-        scatter(last, 0, HALF, C, dx0[:])
+        dx0 = sb.tile([P, C - QUARTER], F32, name="dx0%d" % last, tag="keep10", align_bytes=64)
+        nc.scalar.copy(out=dx0[:], in_=banks0[last][:, QUARTER:])
+        scatter(last, 0, QUARTER, C, dx0[:])
         for c in range(K // P):
             dx1 = sb.tile([P, C], F32, name="dx1%d" % c)
             nc.scalar.copy(out=dx1[:], in_=expert(1, c)[:])

@@ -103,7 +103,7 @@ def tile_moe_sdb_relu_kernel(
         for q in range(2, QUADS):
             load_dy_scales(q, nc.scalar)
         dy_rows = dy_words[0].rearrange("p t d -> p (t d)").bitcast(I32)
-        for tokens in (slice(0, BANK + QUARTER), slice(BANK + QUARTER, T)):
+        for tokens in (slice(0, BANK), slice(BANK, T)):
             nc.sync.dma_start(out=dy_w[:, tokens].bitcast(I32), in_=dy_rows[:, tokens])
         a_planes = a.rearrange("(p t) j -> p t j", t=PACK)
         nc.sync.dma_start(offsets[:], offs)
@@ -162,6 +162,9 @@ def tile_moe_sdb_relu_kernel(
         def woven_half(h):
             return slice(h * HALF * PACK, (h + 1) * HALF * PACK)
 
+        def woven_quarter(u):
+            return slice(u * QUARTER * PACK, (u + 1) * QUARTER * PACK)
+
         def quantise(e, lo, hi, values):
             nc.vector.quantize_mx(out=da_w[e][:, lo:hi].bitcast(E5M2X4), scales=da_s[e][:, lo:hi], in_=values)
 
@@ -212,11 +215,11 @@ def tile_moe_sdb_relu_kernel(
         nc.tensor.transpose(turned[:, 0:P], by_slot_first[:], identity[:])
         by_row_first = sb.tile([P, P], F32, name="by_row_first")
         nc.scalar.copy(out=by_row_first[:], in_=turned[:, 0:P])
-        by_slot_middle = sb.tile([P, 2 * P], F32, name="by_slot_middle")
-        nc.scalar.copy(out=by_slot_middle[:], in_=acc[:, P : 3 * P])
+        by_slot_middle = sb.tile([P, 2 * P], F32, name="by_slot_middle", align_bytes=64)
         nc.scalar.copy(out=by_slot_last, in_=acc[:, 3 * P :])
+        nc.scalar.copy(out=by_slot_middle[:], in_=acc[:, P : 3 * P])
         turned = bank_tile("turned_rest", 2)
-        for j, by_slot in enumerate((by_slot_middle[:, 0:P], by_slot_middle[:, P:], by_slot_last)):
+        for j, by_slot in ((2, by_slot_last), (0, by_slot_middle[:, 0:P]), (1, by_slot_middle[:, P:])):
             nc.tensor.transpose(turned[:, j * P : (j + 1) * P], by_slot, identity[:])
         by_row_rest = sb.tile([P, K - P], F32, name="by_row_rest")
         nc.scalar.copy(out=by_row_rest[:], in_=turned[:, 0 : K - P])
@@ -249,47 +252,47 @@ def tile_moe_sdb_relu_kernel(
             nc.scalar.copy(out=dx0[:], in_=banks0[c][:, QUARTER:])
             scatter(c, 0, QUARTER, C, dx0[:])
 
-        sign1 = [woven_tile("sign10", HALF, "da_s0"), woven_tile("sign11", HALF, "keep01")]
-        keep1 = [woven_tile("keep1%d" % h, HALF) for h in range(2)]
+        sign1 = woven_tile("sign1", C, "by_slot_middle")
+        keep1_first = woven_tile("keep1_first", HALF, "da_s0")
+        keep1_second = woven_tile("keep1_second", HALF)
         gated1 = sb.tile([P, PACK, HALF], F32, name="gated1", tag="after_quantise0", align_bytes=64)
         da1 = woven_tile("da1", C)
-
-        def masks1(h):
-            nc.scalar.activation((woven, by_lines)[h](sign1[h]), planes(a1[:, :, h * HALF : (h + 1) * HALF]), ACT.Sign)
-            nc.scalar.activation(keep1[h], sign1[h], ACT.Relu)
 
         nc.gpsimd.tensor_tensor(
             gated1[:], raw1[:, :, HALF:], gate1_rows.unsqueeze(1).to_broadcast([P, PACK, HALF]), ALU.mult
         )
-        masks1(1)
-        nc.gpsimd.tensor_tensor(woven(da1[:, woven_half(1)]), planes(gated1[:]), by_lines(keep1[1]), ALU.mult)
+        nc.scalar.activation(by_lines(sign1[:, woven_half(1)]), planes(a1[:, :, HALF:]), ACT.Sign)
+        nc.scalar.activation(keep1_second, sign1[:, woven_half(1)], ACT.Relu)
+        nc.scalar.activation(woven(sign1[:, woven_half(0)]), planes(a1[:, :, 0:HALF]), ACT.Sign)
+        nc.gpsimd.tensor_tensor(woven(da1[:, woven_half(1)]), planes(gated1[:]), by_lines(keep1_second), ALU.mult)
         both_pairs = woven_tile("both_pairs", HALF, "da_w0")
-        pairs_by_row = bank_tile("pairs_by_row", PACK)
+        pairs_by_row = []
         for u in range(2):
-            pairs = both_pairs[:, u * PACK * QUARTER : (u + 1) * PACK * QUARTER]
+            pairs = both_pairs[:, woven_quarter(u)]
             nc.scalar.activation(
                 pairs.rearrange("s (w p e) -> s w p e", w=2, e=2),
                 raw_by_slot[:, u * BANK : (u + 1) * BANK].rearrange("s (w e p) -> s w p e", w=2, e=2),
                 ACT.Copy,
                 scale=gate1_columns[:, u : u + 1],
             )
+            pairs_by_row.append(bank_tile("pairs_by_row%d" % u, PACK + u))
             for w in range(2):
-                column = (2 * u + w) * P
                 nc.tensor.transpose(
-                    pairs_by_row[:, column : column + P], pairs.bitcast(F32)[:, w * P : (w + 1) * P], identity[:]
+                    pairs_by_row[u][:, w * P : (w + 1) * P], pairs.bitcast(F32)[:, w * P : (w + 1) * P], identity[:]
                 )
-        rounded1 = woven_tile("rounded1", HALF)
-        nc.scalar.copy(
-            out=rounded1.bitcast(F32).rearrange("p (u s w) -> p u s w", u=2, w=2),
-            in_=pairs_by_row[:].rearrange("p (u w s) -> p u s w", u=2, w=2),
-        )
+        for u in range(2):
+            rounded1 = woven_tile("rounded1%d" % u, QUARTER)
+            nc.scalar.activation(keep1_first[:, woven_quarter(u)], sign1[:, woven_quarter(u)], ACT.Relu)
+            nc.scalar.copy(
+                out=rounded1.bitcast(F32).rearrange("p (s w) -> p s w", w=2),
+                in_=pairs_by_row[u][:, 0:HALF].rearrange("p (w s) -> p s w", w=2),
+            )
+            nc.gpsimd.tensor_tensor(da1[:, woven_quarter(u)], rounded1, keep1_first[:, woven_quarter(u)], ALU.mult)
         dx0 = sb.tile([P, C - QUARTER], F32, name="dx02", tag="da_w0", align_bytes=64)
         nc.scalar.copy(out=dx0[:], in_=banks0[last - 1][:, QUARTER:])
         scatter(last - 1, 0, QUARTER, C, dx0[:])
-        masks1(0)
-        nc.gpsimd.tensor_tensor(da1[:, woven_half(0)], rounded1, keep1[0], ALU.mult)
         quantise(1, 0, C, da1)
-        dx0 = sb.tile([P, C - QUARTER], F32, name="dx0%d" % last, tag="keep10", align_bytes=64)
+        dx0 = sb.tile([P, C - QUARTER], F32, name="dx0%d" % last, tag="da_s0", align_bytes=64)
         nc.scalar.copy(out=dx0[:], in_=banks0[last][:, QUARTER:])
         scatter(last, 0, QUARTER, C, dx0[:])
         for c in range(K // P):

@@ -1,7 +1,6 @@
 from contextlib import ExitStack
 
 import concourse.mybir as mybir
-from concourse.masks import make_identity
 
 K, T, E, C, H, N = 512, 1024, 2, 512, 512, 512
 FLOPS = 2 * N * H * T + 2 * H * K * E * C
@@ -21,10 +20,7 @@ P = 128
 PACK = 4
 QUADS = 4
 BANK = 512
-BANKS = 8
 HALF = C // 2
-QUARTER = C // 4
-EDGE = 32
 LINE = 4
 PER_COLUMN = 16
 
@@ -37,8 +33,8 @@ def tile_moe_sdb_relu_kernel(
         sb = ctx.enter_context(tc.tile_pool(name="sb", bufs=1))
         psum = ctx.enter_context(tc.psum_pool(name="psum", bufs=1))
 
-        def bank_tile(name, first, count=1):
-            return psum.tile([P, count * BANK], F32, name=name, offset=first * BANK * 4)
+        def bank_tile(name, first):
+            return psum.tile([P, BANK], F32, name=name, offset=first * BANK * 4)
 
         offsets = sb.tile([P, E * C // PER_COLUMN], U16, name="offsets")
         dy_w = sb.tile([P, T], U32, name="dy_w", align_bytes=64)
@@ -49,39 +45,14 @@ def tile_moe_sdb_relu_kernel(
         w2_s = sb.tile([P, H], U8, name="w2_s", align_bytes=64)
         w1_w = sb.tile([P, E, 2 * K], U8, name="w1_w", align_bytes=64)
         w1_s = sb.tile([P, E, K], U8, name="w1_s", align_bytes=64)
-        gate0 = sb.tile([P, C], F32, name="gate0")[:]
-        gate1_rows = sb.tile([P, HALF], F32, name="gate1_rows")[:]
-        gate1_columns = sb.tile([P, 2], F32, name="gate1_columns")[:]
-
-        identity = sb.tile([P, P], F32, name="identity")
-        make_identity(nc, identity[:])
-        a0 = [sb.tile([P, PACK, HALF], F32, name="a0%d" % h) for h in range(2)]
-        a1 = sb.tile([P, PACK, C], F32, name="a1")
+        gates = [sb.tile([P, C], F32, name="gate%d" % e) for e in range(E)]
+        a_q = [sb.tile([P, PACK, HALF], F32, name="a%d" % q) for q in range(4)]
         dc = [sb.tile([P, T], F32, name="dc%d" % t) for t in range(PACK)]
-        gated0 = sb.tile([P, PACK, C], F32, name="gated0", align_bytes=64)
-
-        raw1 = sb.tile([P, PACK, C], F32, name="raw1", align_bytes=64)
-        flat1 = raw1[:].rearrange("p t c -> p (t c)")
-        keep_first = flat1[:, 2 * C - QUARTER : 2 * C + QUARTER].bitcast(BF16)
-        sign_first = raw1[:, 2, HALF:].bitcast(BF16)
-
-        def woven_tile(name, slots, tag=None):
-            return sb.tile([P, slots * PACK], BF16, name=name, tag=tag or name, align_bytes=64)[:]
-
-        parts = ((C - QUARTER, C), (QUARTER, HALF - EDGE), (HALF - EDGE, C - QUARTER))
-        sign0_rest = woven_tile("sign0_rest", C - QUARTER)
-        sign0 = [sign_first] + [sign0_rest[:, u * PACK * QUARTER : (u + 1) * PACK * QUARTER] for u in range(3)]
-        keep0 = [raw1[:, 0, 0:HALF].bitcast(BF16)]
-        keep0.extend(woven_tile("keep0%d" % n, parts[n][1] - parts[n][0]) for n in (1, 2))
-        da0 = woven_tile("da0", C - QUARTER, "after_quantise0")
-
-        def rest(ap, lo, hi):
-            return ap[:, PACK * (lo - QUARTER) : PACK * (hi - QUARTER)]
-
-        da0_first = rest(da0, C - QUARTER, C)
-        by_slot_last = rest(da0, HALF, HALF + P // 2).bitcast(F32)
-        da_w = [sb.tile([P, C], U32, name="da_w%d" % e, align_bytes=64) for e in range(E)]
-        da_s = [sb.tile([P, C], U8, name="da_s%d" % e, align_bytes=64) for e in range(E)]
+        gated0 = sb.tile([P, PACK, C], F32, name="gated0")
+        da_w = [sb.tile([P, HALF], U32, name="da_w%d" % q, align_bytes=64) for q in range(4)]
+        da_s = [sb.tile([P, HALF], U8, name="da_s%d" % q, align_bytes=64) for q in range(4)]
+        da = [sb.tile([P, HALF * PACK], BF16, name="da%d" % q, align_bytes=64) for q in range(4)]
+        res = [sb.tile([P, T], F32, name="res%d" % c) for c in range(K // P)]
 
         def scale_partitions(q):
             return slice(32 * q, 32 * q + 4)
@@ -107,19 +78,18 @@ def tile_moe_sdb_relu_kernel(
             nc.sync.dma_start(out=dy_w[:, tokens].bitcast(I32), in_=dy_rows[:, tokens])
         a_planes = a.rearrange("(p t) j -> p t j", t=PACK)
         nc.sync.dma_start(offsets[:], offs)
-        nc.sync.dma_start(out=gate0, in_=gate[:, 0:C])
-        for h in range(2):
-            nc.sync.dma_start(out=a0[h][:], in_=a_planes[:, :, h * HALF : (h + 1) * HALF])
-        nc.sync.dma_start(out=gate1_rows, in_=gate[:, C + HALF : 2 * C])
+        nc.sync.dma_start(out=gates[0][:], in_=gate[:, 0:C])
+        for q in range(2):
+            nc.sync.dma_start(out=a_q[q][:], in_=a_planes[:, :, q * HALF : (q + 1) * HALF])
         nc.sync.dma_start(out=w1_w[:].bitcast(I32), in_=w1t_words[:, 0].rearrange("e p b -> p e b").bitcast(I32))
         for q in range(QUADS):
             nc.sync.dma_start(
                 out=w1_s[scale_partitions(q), :, :].bitcast(I32),
                 in_=w1t_scales[:, 0, scale_rows(q), :].rearrange("e r k -> r e k").bitcast(I32),
             )
-        nc.sync.dma_start(out=a1[:], in_=a_planes[:, :, C : 2 * C])
-        with nc.allow_non_contiguous_dma(reason="256 gates, one slot on each partition"):
-            nc.sync.dma_start(out=gate1_columns, in_=gate[0, C : C + HALF].rearrange("(q p) -> p q", p=P))
+        nc.sync.dma_start(out=gates[1][:], in_=gate[:, C : 2 * C])
+        for q in range(2, 4):
+            nc.sync.dma_start(out=a_q[q][:], in_=a_planes[:, :, q * HALF : (q + 1) * HALF])
 
         w_src = w2_raw_w[:].bitcast(U16).rearrange("p (m t) -> p t m", t=PACK)
         w_dst = w2_w[:].bitcast(U16).rearrange("p (t m) -> p t m", t=PACK)
@@ -147,8 +117,11 @@ def tile_moe_sdb_relu_kernel(
                 else:
                     nc.scalar.activation(dc[t][:, tokens], acc[:], ACT.Copy)
 
-        def entries(e, lo, hi):
-            return offsets[:, (e * C + lo) // PER_COLUMN : (e * C + hi) // PER_COLUMN]
+        def entries(lo, hi):
+            return offsets[:, lo // PER_COLUMN : hi // PER_COLUMN]
+
+        def half(h):
+            return slice(h * HALF, (h + 1) * HALF)
 
         def woven(ap):
             return ap.rearrange("p (c i t) -> p c t i", i=LINE, t=PACK)
@@ -156,147 +129,102 @@ def tile_moe_sdb_relu_kernel(
         def planes(ap):
             return ap.rearrange("p t (c i) -> p c t i", i=LINE)
 
-        def by_lines(ap):
-            return ap.rearrange("p (c t i) -> p c t i", i=LINE, t=PACK)
+        def quantise(q):
+            nc.vector.quantize_mx(out=da_w[q][:].bitcast(E5M2X4), scales=da_s[q][:], in_=da[q][:])
 
-        def woven_half(h):
-            return slice(h * HALF * PACK, (h + 1) * HALF * PACK)
+        def gather_gated(t, lo, hi):
+            nc.vector.tensor_tensor(gated0[:, t, lo:hi], dc[t][:].indirect(entries(lo, hi)), gates[0][:, lo:hi], ALU.mult)
 
-        def woven_quarter(u):
-            return slice(u * QUARTER * PACK, (u + 1) * QUARTER * PACK)
-
-        def quantise(e, lo, hi, values):
-            nc.vector.quantize_mx(out=da_w[e][:, lo:hi].bitcast(E5M2X4), scales=da_s[e][:, lo:hi], in_=values)
-
-        def expert(e, c):
-            acc = bank_tile("dx_acc%d%d" % (e, c), c + PACK * (1 - e))
-            nc.tensor.matmul_mx(
-                out=acc[:],
-                lhsT=w1_w[:, e, 2 * P * c : 2 * P * (c + 1)].bitcast(E2M1X4),
-                lhsT_scale=w1_s[:, e, P * c : P * (c + 1)],
-                rhs=da_w[e][:].bitcast(E5M2X4),
-                rhs_scale=da_s[e][:],
-                start=True,
-                stop=True,
+        def mask0(h):
+            nc.vector.scalar_tensor_tensor(
+                out=da[h][:].rearrange("p (c t) -> p c t", t=PACK),
+                in0=a_q[h][:].rearrange("p t c -> p c t"),
+                scalar=0.0,
+                in1=gated0[:, :, half(h)].rearrange("p t c -> p c t"),
+                op0=ALU.is_gt,
+                op1=ALU.mult,
             )
-            return acc
 
-        def scatter(c, e, lo, hi, values):
-            nc.vector.tensor_copy(res[c][:].indirect(entries(e, lo, hi)), values)
+        def expert(q):
+            e = q // 2
+            pieces = []
+            for pair in range(2):
+                acc = bank_tile("dx_acc%d%d" % (q, pair), (5 + 2 * q + pair) % 8)
+                for j in range(2):
+                    c = 2 * pair + j
+                    nc.tensor.matmul_mx(
+                        out=acc[:, half(j)],
+                        lhsT=w1_w[:, e, 2 * P * c : 2 * P * (c + 1)].bitcast(E2M1X4),
+                        lhsT_scale=w1_s[:, e, P * c : P * (c + 1)],
+                        rhs=da_w[q][:].bitcast(E5M2X4),
+                        rhs_scale=da_s[q][:],
+                        start=True,
+                        stop=True,
+                    )
+                dx = sb.tile([P, BANK], F32, name="dx%d%d" % (q, pair))
+                nc.scalar.copy(out=dx[:], in_=acc[:])
+                pieces.extend(dx[:, half(j)] for j in range(2))
+            return pieces
 
-        def quarter(u):
-            return slice(u * QUARTER, (u + 1) * QUARTER)
+        def scatter_scalar(q, c, values):
+            nc.scalar.activation(res[c][:].indirect(entries(q * HALF, (q + 1) * HALF)), values, ACT.Copy)
 
-        def signs0(u):
-            nc.scalar.activation(by_lines(sign0[u]), planes(a0[u // 2][:, :, quarter(u % 2)]), ACT.Sign)
+        def scatter_vector(q, c, values):
+            nc.vector.tensor_copy(res[c][:].indirect(entries(q * HALF, (q + 1) * HALF)), values)
 
+        for t in range(PACK - 1):
+            gather_gated(t, 0, C)
+        raw1 = sb.tile([P, PACK, C], F32, name="raw1", tag="dy_w", align_bytes=64)
         for t in range(PACK):
-            nc.vector.tensor_tensor(gated0[:, t, :], dc[t][:].indirect(entries(0, 0, C)), gate0, ALU.mult)
-        nc.vector.tensor_copy(raw1[:, 3, :], dc[3][:].indirect(entries(1, 0, C)))
+            nc.scalar.activation(raw1[:, t, :], dc[t][:].indirect(entries(C, 2 * C)), ACT.Copy)
 
-        signs0(0)
-        nc.scalar.activation(keep_first, sign0[0], ACT.Relu)
-        nc.gpsimd.tensor_tensor(woven(da0_first), planes(gated0[:, :, quarter(0)]), by_lines(keep_first), ALU.mult)
-        nc.vector.tensor_copy(raw1[:, 2, HALF:], dc[2][:].indirect(entries(1, HALF, C)))
-        quantise(0, 0, QUARTER, da0_first)
-        acc = bank_tile("early_acc", 0)
-        nc.tensor.matmul_mx(
-            out=acc[:],
-            lhsT=da_w[0][:, quarter(0)].bitcast(E5M2X4),
-            lhsT_scale=da_s[0][:, quarter(0)],
-            rhs=w1_w[:, 0, :].bitcast(E2M1X4),
-            rhs_scale=w1_s[:, 0, :],
-            start=True,
-            stop=True,
-        )
-        by_slot_first = sb.tile([P, P], F32, name="by_slot_first")
-        nc.scalar.copy(out=by_slot_first[:], in_=acc[:, 0:P])
-        turned = bank_tile("turned_first", 1)
-        nc.tensor.transpose(turned[:, 0:P], by_slot_first[:], identity[:])
-        by_row_first = sb.tile([P, P], F32, name="by_row_first")
-        nc.scalar.copy(out=by_row_first[:], in_=turned[:, 0:P])
-        by_slot_middle = sb.tile([P, 2 * P], F32, name="by_slot_middle", align_bytes=64)
-        nc.scalar.copy(out=by_slot_last, in_=acc[:, 3 * P :])
-        nc.scalar.copy(out=by_slot_middle[:], in_=acc[:, P : 3 * P])
-        turned = bank_tile("turned_rest", 2)
-        for j, by_slot in ((2, by_slot_last), (0, by_slot_middle[:, 0:P]), (1, by_slot_middle[:, P:])):
-            nc.tensor.transpose(turned[:, j * P : (j + 1) * P], by_slot, identity[:])
-        by_row_rest = sb.tile([P, K - P], F32, name="by_row_rest")
-        nc.scalar.copy(out=by_row_rest[:], in_=turned[:, 0 : K - P])
-        dx_first = [by_row_first[:]] + [by_row_rest[:, j * P : (j + 1) * P] for j in range(3)]
-        nc.vector.tensor_copy(raw1[:, 2, 0:HALF], dc[2][:].indirect(entries(1, 0, HALF)))
-        nc.vector.tensor_copy(raw1[:, 1, :], dc[1][:].indirect(entries(1, 0, C)))
+        dx = []
+        gather_gated(PACK - 1, 0, HALF)
+        mask0(0)
+        gather_gated(PACK - 1, HALF, C)
+        quantise(0)
+        dx.append(expert(0))
+        mask0(1)
+        factor = []
 
-        for u, keep, (lo, hi) in zip((3, 1, 2), keep0, parts):
-            signs0(u)
-            nc.scalar.activation(keep, rest(sign0_rest, lo, hi), ACT.Relu)
-            nc.gpsimd.tensor_tensor(woven(rest(da0, lo, hi)), planes(gated0[:, :, lo:hi]), by_lines(keep), ALU.mult)
-        nc.vector.tensor_copy(raw1[:, 0, :], dc[0][:].indirect(entries(1, 0, C)))
-        last = K // P - 1
-        res = [sb.tile([P, T], F32, name="res%d" % c) for c in range(2)]
+        def gate_mask(h):
+            factor.append(sb.tile([P, PACK, HALF], F32, name="factor%d" % h, tag="a%d" % h))
+            nc.vector.scalar_tensor_tensor(
+                out=factor[h][:],
+                in0=a_q[2 + h][:],
+                scalar=0.0,
+                in1=gates[1][:, half(h)].unsqueeze(1).to_broadcast([P, PACK, HALF]),
+                op0=ALU.is_gt,
+                op1=ALU.mult,
+            )
+
+        def product1(h):
+            nc.vector.tensor_tensor(woven(da[2 + h][:]), planes(raw1[:, :, half(h)]), planes(factor[h][:]), ALU.mult)
+
+        gate_mask(0)
+        quantise(1)
         for c in range(2):
-            scatter(c, 0, 0, QUARTER, dx_first[c])
-        quantise(0, QUARTER, HALF, rest(da0, QUARTER, HALF))
-        quantise(0, HALF, C, rest(da0, HALF, C))
-        for c, tag in ((2, "gated0"), (3, "keep02")):
-            res.append(sb.tile([P, T], F32, name="res%d" % c, tag=tag, align_bytes=64))
-            scatter(c, 0, 0, QUARTER, dx_first[c])
-        raw_by_slot = bank_tile("raw_by_slot", 2, 2)
-        for u in range(2):
-            for t in range(PACK):
-                column = u * BANK + t * P
-                nc.tensor.transpose(raw_by_slot[:, column : column + P], raw1[:, t, quarter(u)], identity[:])
-        banks0 = [expert(0, c) for c in range(K // P)]
-        for c in range(last - 1):
-            dx0 = sb.tile([P, C - QUARTER], F32, name="dx0%d" % c)
-            nc.scalar.copy(out=dx0[:], in_=banks0[c][:, QUARTER:])
-            scatter(c, 0, QUARTER, C, dx0[:])
-
-        sign1 = woven_tile("sign1", C, "by_slot_middle")
-        keep1_first = woven_tile("keep1_first", HALF, "da_s0")
-        keep1_second = woven_tile("keep1_second", HALF)
-        gated1 = sb.tile([P, PACK, HALF], F32, name="gated1", tag="after_quantise0", align_bytes=64)
-        da1 = woven_tile("da1", C)
-
-        nc.gpsimd.tensor_tensor(
-            gated1[:], raw1[:, :, HALF:], gate1_rows.unsqueeze(1).to_broadcast([P, PACK, HALF]), ALU.mult
-        )
-        nc.scalar.activation(by_lines(sign1[:, woven_half(1)]), planes(a1[:, :, HALF:]), ACT.Sign)
-        nc.scalar.activation(keep1_second, sign1[:, woven_half(1)], ACT.Relu)
-        nc.scalar.activation(woven(sign1[:, woven_half(0)]), planes(a1[:, :, 0:HALF]), ACT.Sign)
-        nc.gpsimd.tensor_tensor(woven(da1[:, woven_half(1)]), planes(gated1[:]), by_lines(keep1_second), ALU.mult)
-        both_pairs = woven_tile("both_pairs", HALF, "da_w0")
-        pairs_by_row = []
-        for u in range(2):
-            pairs = both_pairs[:, woven_quarter(u)]
-            nc.scalar.activation(
-                pairs.rearrange("s (w p e) -> s w p e", w=2, e=2),
-                raw_by_slot[:, u * BANK : (u + 1) * BANK].rearrange("s (w e p) -> s w p e", w=2, e=2),
-                ACT.Copy,
-                scale=gate1_columns[:, u : u + 1],
-            )
-            pairs_by_row.append(bank_tile("pairs_by_row%d" % u, PACK + u))
-            for w in range(2):
-                nc.tensor.transpose(
-                    pairs_by_row[u][:, w * P : (w + 1) * P], pairs.bitcast(F32)[:, w * P : (w + 1) * P], identity[:]
-                )
-        for u in range(2):
-            rounded1 = woven_tile("rounded1%d" % u, QUARTER)
-            nc.scalar.activation(keep1_first[:, woven_quarter(u)], sign1[:, woven_quarter(u)], ACT.Relu)
-            nc.scalar.copy(
-                out=rounded1.bitcast(F32).rearrange("p (s w) -> p s w", w=2),
-                in_=pairs_by_row[u][:, 0:HALF].rearrange("p (w s) -> p s w", w=2),
-            )
-            nc.gpsimd.tensor_tensor(da1[:, woven_quarter(u)], rounded1, keep1_first[:, woven_quarter(u)], ALU.mult)
-        dx0 = sb.tile([P, C - QUARTER], F32, name="dx02", tag="da_w0", align_bytes=64)
-        nc.scalar.copy(out=dx0[:], in_=banks0[last - 1][:, QUARTER:])
-        scatter(last - 1, 0, QUARTER, C, dx0[:])
-        quantise(1, 0, C, da1)
-        dx0 = sb.tile([P, C - QUARTER], F32, name="dx0%d" % last, tag="da_s0", align_bytes=64)
-        nc.scalar.copy(out=dx0[:], in_=banks0[last][:, QUARTER:])
-        scatter(last, 0, QUARTER, C, dx0[:])
-        for c in range(K // P):
-            dx1 = sb.tile([P, C], F32, name="dx1%d" % c)
-            nc.scalar.copy(out=dx1[:], in_=expert(1, c)[:])
-            scatter(c, 1, 0, C, dx1[:])
-            nc.sync.dma_start(out=out[c * P : (c + 1) * P, :], in_=res[c][:])
+            scatter_scalar(0, c, dx[0][c])
+        dx.append(expert(1))
+        product1(0)
+        gate_mask(1)
+        quantise(2)
+        for c in range(2):
+            scatter_scalar(1, c, dx[1][c])
+        dx.append(expert(2))
+        product1(1)
+        scatter_vector(0, 2, dx[0][2])
+        quantise(3)
+        scatter_scalar(2, 0, dx[2][0])
+        dx.append(expert(3))
+        scatter_scalar(3, 0, dx[3][0])
+        nc.sync.dma_start(out=out[0:P, :], in_=res[0][:])
+        for q in range(1, 4):
+            scatter_vector(q, 2, dx[q][2])
+        nc.sync.dma_start(out=out[2 * P : 3 * P, :], in_=res[2][:])
+        for q in range(4):
+            scatter_vector(q, 3, dx[q][3])
+        for q in range(2, 4):
+            scatter_scalar(q, 1, dx[q][1])
+        nc.sync.dma_start(out=out[P : 2 * P, :], in_=res[1][:])
+        nc.sync.dma_start(out=out[3 * P : 4 * P, :], in_=res[3][:])

@@ -21,7 +21,7 @@ PACK = 4
 QUADS = 4
 BANK = 512
 HALF = C // 2
-LINE = 4
+LINE = 2
 PER_COLUMN = 16
 
 
@@ -45,14 +45,20 @@ def tile_moe_sdb_relu_kernel(
         w2_s = sb.tile([P, H], U8, name="w2_s", align_bytes=64)
         w1_w = sb.tile([P, E, 2 * K], U8, name="w1_w", align_bytes=64)
         w1_s = sb.tile([P, E, K], U8, name="w1_s", align_bytes=64)
-        gates = [sb.tile([P, C], F32, name="gate%d" % e) for e in range(E)]
+        shared = sb.tile([P, 2 * C], F32, name="shared")
+        gates = [shared[:, 0:C], sb.tile([P, C], F32, name="gate1")[:]]
         a_q = [sb.tile([P, PACK, HALF], F32, name="a%d" % q) for q in range(4)]
         dc = [sb.tile([P, T], F32, name="dc%d" % t) for t in range(PACK)]
-        gated0 = sb.tile([P, PACK, C], F32, name="gated0")
+        gated_low = sb.tile([P, 2, C], F32, name="gated_low")
+        gated_high = sb.tile([P, 2, HALF], F32, name="gated_high")
+        gated = [
+            [gated_low[:, :, 0:HALF], gated_high[:]],
+            [gated_low[:, :, HALF:C], shared[:].rearrange("p (e c) -> p e c", e=2)[:, :, 0:HALF]],
+        ]
         da_w = [sb.tile([P, HALF], U32, name="da_w%d" % q, align_bytes=64) for q in range(4)]
         da_s = [sb.tile([P, HALF], U8, name="da_s%d" % q, align_bytes=64) for q in range(4)]
-        da = [sb.tile([P, HALF * PACK], BF16, name="da%d" % q, align_bytes=64) for q in range(4)]
-        res = [sb.tile([P, T], F32, name="res%d" % c) for c in range(K // P)]
+        da = [sb.tile([P, HALF * PACK], BF16, name="da%d" % q, align_bytes=64) for q in range(3)]
+        res = [sb.tile([P, T], F32, name="res%d" % c) for c in range(2)]
 
         def scale_partitions(q):
             return slice(32 * q, 32 * q + 4)
@@ -78,7 +84,7 @@ def tile_moe_sdb_relu_kernel(
             nc.sync.dma_start(out=dy_w[:, tokens].bitcast(I32), in_=dy_rows[:, tokens])
         a_planes = a.rearrange("(p t) j -> p t j", t=PACK)
         nc.sync.dma_start(offsets[:], offs)
-        nc.sync.dma_start(out=gates[0][:], in_=gate[:, 0:C])
+        nc.sync.dma_start(out=gates[0], in_=gate[:, 0:C])
         for q in range(2):
             nc.sync.dma_start(out=a_q[q][:], in_=a_planes[:, :, q * HALF : (q + 1) * HALF])
         nc.sync.dma_start(out=w1_w[:].bitcast(I32), in_=w1t_words[:, 0].rearrange("e p b -> p e b").bitcast(I32))
@@ -87,7 +93,7 @@ def tile_moe_sdb_relu_kernel(
                 out=w1_s[scale_partitions(q), :, :].bitcast(I32),
                 in_=w1t_scales[:, 0, scale_rows(q), :].rearrange("e r k -> r e k").bitcast(I32),
             )
-        nc.sync.dma_start(out=gates[1][:], in_=gate[:, C : 2 * C])
+        nc.sync.dma_start(out=gates[1], in_=gate[:, C : 2 * C])
         for q in range(2, 4):
             nc.sync.dma_start(out=a_q[q][:], in_=a_planes[:, :, q * HALF : (q + 1) * HALF])
 
@@ -132,17 +138,28 @@ def tile_moe_sdb_relu_kernel(
         def quantise(q):
             nc.vector.quantize_mx(out=da_w[q][:].bitcast(E5M2X4), scales=da_s[q][:], in_=da[q][:])
 
-        def gather_gated(t, lo, hi):
-            nc.vector.tensor_tensor(gated0[:, t, lo:hi], dc[t][:].indirect(entries(lo, hi)), gates[0][:, lo:hi], ALU.mult)
+        def gather_gated(values, t, lo, hi):
+            nc.vector.tensor_tensor(values, dc[t][:].indirect(entries(lo, hi)), gates[0][:, lo:hi], ALU.mult)
 
-        def mask0(h):
+        def gather_high(t, h):
+            gather_gated(gated[h][1][:, t - 2, :], t, h * HALF, (h + 1) * HALF)
+
+        pairs = [sb.tile([P, 2, 2 * HALF], BF16, name="pairs0", align_bytes=64)]
+
+        def mask0(h, w):
             nc.vector.scalar_tensor_tensor(
-                out=da[h][:].rearrange("p (c t) -> p c t", t=PACK),
-                in0=a_q[h][:].rearrange("p t c -> p c t"),
+                out=pairs[h][:, w, :].rearrange("p (c e) -> p c e", e=2),
+                in0=a_q[h][:, 2 * w : 2 * w + 2, :].rearrange("p e c -> p c e"),
                 scalar=0.0,
-                in1=gated0[:, :, half(h)].rearrange("p t c -> p c t"),
+                in1=gated[h][w].rearrange("p e c -> p c e"),
                 op0=ALU.is_gt,
                 op1=ALU.mult,
+            )
+
+        def weave0(h):
+            nc.vector.tensor_copy(
+                out=da[h][:].bitcast(F32).rearrange("p (c w) -> p c w", w=2),
+                in_=pairs[h][:].bitcast(F32).rearrange("p w c -> p c w"),
             )
 
         def expert(q):
@@ -172,59 +189,68 @@ def tile_moe_sdb_relu_kernel(
         def scatter_vector(q, c, values):
             nc.vector.tensor_copy(res[c][:].indirect(entries(q * HALF, (q + 1) * HALF)), values)
 
-        for t in range(PACK - 1):
-            gather_gated(t, 0, C)
+        for t in range(2):
+            gather_gated(gated_low[:, t, :], t, 0, C)
+        gather_high(2, 0)
+        mask0(0, 0)
         raw1 = sb.tile([P, PACK, C], F32, name="raw1", tag="dy_w", align_bytes=64)
         for t in range(PACK):
             nc.scalar.activation(raw1[:, t, :], dc[t][:].indirect(entries(C, 2 * C)), ACT.Copy)
 
+        def gate_rows(h):
+            return gates[1][:, half(h)].unsqueeze(1).to_broadcast([P, PACK, HALF])
+
         dx = []
-        gather_gated(PACK - 1, 0, HALF)
-        mask0(0)
-        gather_gated(PACK - 1, HALF, C)
+        gather_high(3, 0)
+        gather_high(3, 1)
+        mask0(0, 1)
+        gather_high(2, 1)
+        weave0(0)
+        pairs.append(sb.tile([P, 2, 2 * HALF], BF16, name="pairs1", tag="a0"))
+        mask0(1, 0)
         quantise(0)
         dx.append(expert(0))
-        mask0(1)
+        mask0(1, 1)
         factor = []
 
         def gate_mask(h):
-            factor.append(sb.tile([P, PACK, HALF], F32, name="factor%d" % h, tag="a%d" % h))
+            factor.append(sb.tile([P, PACK, HALF], F32, name="factor%d" % h, tag=("pairs0", "da0")[h], align_bytes=64))
             nc.vector.scalar_tensor_tensor(
-                out=factor[h][:],
-                in0=a_q[2 + h][:],
-                scalar=0.0,
-                in1=gates[1][:, half(h)].unsqueeze(1).to_broadcast([P, PACK, HALF]),
-                op0=ALU.is_gt,
-                op1=ALU.mult,
+                out=factor[h][:], in0=a_q[2 + h][:], scalar=0.0, in1=gate_rows(h), op0=ALU.is_gt, op1=ALU.mult
             )
 
-        def product1(h):
-            nc.vector.tensor_tensor(woven(da[2 + h][:]), planes(raw1[:, :, half(h)]), planes(factor[h][:]), ALU.mult)
+        def product1(h, engine):
+            engine.tensor_tensor(woven(da[2 + h][:]), planes(raw1[:, :, half(h)]), planes(factor[h][:]), ALU.mult)
 
         gate_mask(0)
+        weave0(1)
+        product1(0, nc.vector)
         quantise(1)
         for c in range(2):
             scatter_scalar(0, c, dx[0][c])
         dx.append(expert(1))
-        product1(0)
         gate_mask(1)
         quantise(2)
-        for c in range(2):
-            scatter_scalar(1, c, dx[1][c])
+        da.append(sb.tile([P, HALF * PACK], BF16, name="da3", tag="da2", align_bytes=64))
+        product1(1, nc.gpsimd)
+        res.append(sb.tile([P, T], F32, name="res2", tag="da1", align_bytes=64))
+        scatter_scalar(1, 0, dx[1][0])
         dx.append(expert(2))
-        product1(1)
-        scatter_vector(0, 2, dx[0][2])
+        for q in range(3):
+            scatter_vector(q, 2, dx[q][2])
         quantise(3)
-        scatter_scalar(2, 0, dx[2][0])
+        res.append(sb.tile([P, T], F32, name="res3", tag="da2", align_bytes=64))
+        for c in range(2):
+            scatter_scalar(2, c, dx[2][c])
         dx.append(expert(3))
         scatter_scalar(3, 0, dx[3][0])
         nc.sync.dma_start(out=out[0:P, :], in_=res[0][:])
-        for q in range(1, 4):
-            scatter_vector(q, 2, dx[q][2])
+        for q, c in ((0, 3), (1, 3), (3, 2)):
+            scatter_vector(q, c, dx[q][c])
         nc.sync.dma_start(out=out[2 * P : 3 * P, :], in_=res[2][:])
-        for q in range(4):
-            scatter_vector(q, 3, dx[q][3])
-        for q in range(2, 4):
+        for q in (3, 1):
             scatter_scalar(q, 1, dx[q][1])
         nc.sync.dma_start(out=out[P : 2 * P, :], in_=res[1][:])
+        for q in (3, 2):
+            scatter_vector(q, 3, dx[q][3])
         nc.sync.dma_start(out=out[3 * P : 4 * P, :], in_=res[3][:])

@@ -162,32 +162,36 @@ def tile_moe_sdb_relu_kernel(
                 in_=pairs[h][:].bitcast(F32).rearrange("p w c -> p c w"),
             )
 
-        def expert(q):
+        dx = [sb.tile([P, 2, E * C], F32, name="dx%d" % pair) for pair in range(2)]
+
+        def expert(q, pair):
             e = q // 2
-            pieces = []
-            for pair in range(2):
-                acc = bank_tile("dx_acc%d%d" % (q, pair), (5 + 2 * q + pair) % 8)
-                for j in range(2):
-                    c = 2 * pair + j
-                    nc.tensor.matmul_mx(
-                        out=acc[:, half(j)],
-                        lhsT=w1_w[:, e, 2 * P * c : 2 * P * (c + 1)].bitcast(E2M1X4),
-                        lhsT_scale=w1_s[:, e, P * c : P * (c + 1)],
-                        rhs=da_w[q][:].bitcast(E5M2X4),
-                        rhs_scale=da_s[q][:],
-                        start=True,
-                        stop=True,
-                    )
-                dx = sb.tile([P, BANK], F32, name="dx%d%d" % (q, pair))
-                nc.scalar.copy(out=dx[:], in_=acc[:])
-                pieces.extend(dx[:, half(j)] for j in range(2))
-            return pieces
+            acc = bank_tile("dx_acc%d%d" % (q, pair), (5 + 2 * q + pair) % 8)
+            for j in range(2):
+                c = 2 * pair + j
+                nc.tensor.matmul_mx(
+                    out=acc[:, half(j)],
+                    lhsT=w1_w[:, e, 2 * P * c : 2 * P * (c + 1)].bitcast(E2M1X4),
+                    lhsT_scale=w1_s[:, e, P * c : P * (c + 1)],
+                    rhs=da_w[q][:].bitcast(E5M2X4),
+                    rhs_scale=da_s[q][:],
+                    start=True,
+                    stop=True,
+                )
+            return acc[:].rearrange("p (j s) -> p j s", j=2)
 
-        def scatter_scalar(q, c, values):
-            nc.scalar.activation(res[c][:].indirect(entries(q * HALF, (q + 1) * HALF)), values, ACT.Copy)
+        def empty_scalar(q, pair):
+            nc.scalar.copy(out=dx[pair][:, :, half(q)], in_=expert(q, pair))
 
-        def scatter_vector(q, c, values):
-            nc.vector.tensor_copy(res[c][:].indirect(entries(q * HALF, (q + 1) * HALF)), values)
+        def empty_vector(q, pair):
+            nc.vector.tensor_copy(out=dx[pair][:, :, half(q)], in_=expert(q, pair))
+
+        def scatter_scalar(c, q):
+            nc.scalar.activation(res[c][:].indirect(entries(q * HALF, (q + 1) * HALF)), dx[0][:, c, half(q)], ACT.Copy)
+
+        def scatter_vector(c, first, last):
+            lo, hi = first * HALF, (last + 1) * HALF
+            nc.vector.tensor_copy(res[c][:].indirect(entries(lo, hi)), dx[1][:, c - 2, lo:hi])
 
         for t in range(2):
             gather_gated(gated_low[:, t, :], t, 0, C)
@@ -200,7 +204,6 @@ def tile_moe_sdb_relu_kernel(
         def gate_rows(h):
             return gates[1][:, half(h)].unsqueeze(1).to_broadcast([P, PACK, HALF])
 
-        dx = []
         gather_high(3, 0)
         gather_high(3, 1)
         mask0(0, 1)
@@ -209,48 +212,45 @@ def tile_moe_sdb_relu_kernel(
         pairs.append(sb.tile([P, 2, 2 * HALF], BF16, name="pairs1", tag="a0"))
         mask0(1, 0)
         quantise(0)
-        dx.append(expert(0))
+        for pair in range(2):
+            empty_scalar(0, pair)
         mask0(1, 1)
-        factor = []
-
-        def gate_mask(h):
-            factor.append(sb.tile([P, PACK, HALF], F32, name="factor%d" % h, tag=("pairs0", "da0")[h], align_bytes=64))
-            nc.vector.scalar_tensor_tensor(
-                out=factor[h][:], in0=a_q[2 + h][:], scalar=0.0, in1=gate_rows(h), op0=ALU.is_gt, op1=ALU.mult
-            )
-
-        def product1(h, engine):
-            engine.tensor_tensor(woven(da[2 + h][:]), planes(raw1[:, :, half(h)]), planes(factor[h][:]), ALU.mult)
-
-        gate_mask(0)
+        factor2 = sb.tile([P, PACK, HALF], F32, name="factor2", tag="pairs0", align_bytes=64)
+        nc.vector.scalar_tensor_tensor(
+            out=factor2[:], in0=a_q[2][:], scalar=0.0, in1=gate_rows(0), op0=ALU.is_gt, op1=ALU.mult
+        )
         weave0(1)
-        product1(0, nc.vector)
+        nc.vector.tensor_tensor(woven(da[2][:]), planes(raw1[:, :, half(0)]), planes(factor2[:]), ALU.mult)
         quantise(1)
         for c in range(2):
-            scatter_scalar(0, c, dx[0][c])
-        dx.append(expert(1))
-        gate_mask(1)
+            scatter_scalar(c, 0)
+        for pair in (1, 0):
+            empty_scalar(1, pair)
+        keep3 = sb.tile([P, PACK, HALF], BF16, name="keep3", tag="a0")
+        nc.vector.tensor_scalar(keep3[:], a_q[3][:], 0.0, None, op0=ALU.is_gt)
         quantise(2)
-        da.append(sb.tile([P, HALF * PACK], BF16, name="da3", tag="da2", align_bytes=64))
-        product1(1, nc.gpsimd)
+        factor3 = sb.tile([P, PACK, HALF], F32, name="factor3", tag="da2", align_bytes=64)
+        nc.gpsimd.tensor_tensor(factor3[:], keep3[:], gate_rows(1), ALU.mult)
+        da.append(sb.tile([P, HALF * PACK], BF16, name="da3", align_bytes=64))
+        nc.gpsimd.tensor_tensor(woven(da[3][:]), planes(raw1[:, :, half(1)]), planes(factor3[:]), ALU.mult)
         res.append(sb.tile([P, T], F32, name="res2", tag="da1", align_bytes=64))
-        scatter_scalar(1, 0, dx[1][0])
-        dx.append(expert(2))
-        for q in range(3):
-            scatter_vector(q, 2, dx[q][2])
-        quantise(3)
-        res.append(sb.tile([P, T], F32, name="res3", tag="da2", align_bytes=64))
+        scatter_vector(2, 0, 0)
         for c in range(2):
-            scatter_scalar(2, c, dx[2][c])
-        dx.append(expert(3))
-        scatter_scalar(3, 0, dx[3][0])
-        nc.sync.dma_start(out=out[0:P, :], in_=res[0][:])
-        for q, c in ((0, 3), (1, 3), (3, 2)):
-            scatter_vector(q, c, dx[q][c])
+            scatter_scalar(c, 1)
+        empty_vector(2, 1)
+        empty_scalar(2, 0)
+        scatter_vector(2, 1, 2)
+        quantise(3)
+        res.append(sb.tile([P, T], F32, name="res3", tag="da3", align_bytes=64))
+        for c in range(2):
+            scatter_scalar(c, 2)
+        for pair in (1, 0):
+            empty_scalar(3, pair)
+        scatter_vector(3, 0, 1)
+        scatter_vector(2, 3, 3)
         nc.sync.dma_start(out=out[2 * P : 3 * P, :], in_=res[2][:])
-        for q in (3, 1):
-            scatter_scalar(q, 1, dx[q][1])
-        nc.sync.dma_start(out=out[P : 2 * P, :], in_=res[1][:])
-        for q in (3, 2):
-            scatter_vector(q, 3, dx[q][3])
+        for c in range(2):
+            scatter_scalar(c, 3)
+            nc.sync.dma_start(out=out[c * P : (c + 1) * P, :], in_=res[c][:])
+        scatter_vector(3, 2, 3)
         nc.sync.dma_start(out=out[3 * P : 4 * P, :], in_=res[3][:])

@@ -21,6 +21,7 @@ PACK = 4
 QUADS = 4
 BANK = 512
 HALF = C // 2
+WIDE = 384
 LINE = 2
 PER_COLUMN = 16
 
@@ -45,16 +46,12 @@ def tile_moe_sdb_relu_kernel(
         w2_s = sb.tile([P, H], U8, name="w2_s", align_bytes=64)
         w1_w = sb.tile([P, E, 2 * K], U8, name="w1_w", align_bytes=64)
         w1_s = sb.tile([P, E, K], U8, name="w1_s", align_bytes=64)
-        shared = sb.tile([P, 2 * C], F32, name="shared")
-        gates = [shared[:, 0:C], sb.tile([P, C], F32, name="gate1")[:]]
+        gated = [sb.tile([P, PACK, HALF], F32, name="gated%d" % h) for h in range(2)]
+        across = gated[1][:].rearrange("p t c -> p (t c)")[:, HALF + HALF // 2 : 2 * HALF + HALF // 2]
+        gate0 = [across, sb.tile([P, HALF], F32, name="gate01")[:]]
+        gate1 = sb.tile([P, C], F32, name="gate1")[:]
         a_q = [sb.tile([P, PACK, HALF], F32, name="a%d" % q) for q in range(4)]
         dc = [sb.tile([P, T], F32, name="dc%d" % t) for t in range(PACK)]
-        gated_low = sb.tile([P, 2, C], F32, name="gated_low")
-        gated_high = sb.tile([P, 2, HALF], F32, name="gated_high")
-        gated = [
-            [gated_low[:, :, 0:HALF], gated_high[:]],
-            [gated_low[:, :, HALF:C], shared[:].rearrange("p (e c) -> p e c", e=2)[:, :, 0:HALF]],
-        ]
         da_w = [sb.tile([P, HALF], U32, name="da_w%d" % q, align_bytes=64) for q in range(4)]
         da_s = [sb.tile([P, HALF], U8, name="da_s%d" % q, align_bytes=64) for q in range(4)]
         da = [sb.tile([P, HALF * PACK], BF16, name="da%d" % q, align_bytes=64) for q in range(3)]
@@ -84,18 +81,22 @@ def tile_moe_sdb_relu_kernel(
             nc.sync.dma_start(out=dy_w[:, tokens].bitcast(I32), in_=dy_rows[:, tokens])
         a_planes = a.rearrange("(p t) j -> p t j", t=PACK)
         nc.sync.dma_start(offsets[:], offs)
-        nc.sync.dma_start(out=gates[0], in_=gate[:, 0:C])
-        for q in range(2):
+        for h in range(2):
+            nc.sync.dma_start(out=gate0[h], in_=gate[:, h * HALF : (h + 1) * HALF])
+
+        def load_a(q):
             nc.sync.dma_start(out=a_q[q][:], in_=a_planes[:, :, q * HALF : (q + 1) * HALF])
+
+        nc.sync.dma_start(out=gate1, in_=gate[:, C : 2 * C])
+        for q in (2, 0, 1):
+            load_a(q)
         nc.sync.dma_start(out=w1_w[:].bitcast(I32), in_=w1t_words[:, 0].rearrange("e p b -> p e b").bitcast(I32))
         for q in range(QUADS):
             nc.sync.dma_start(
                 out=w1_s[scale_partitions(q), :, :].bitcast(I32),
                 in_=w1t_scales[:, 0, scale_rows(q), :].rearrange("e r k -> r e k").bitcast(I32),
             )
-        nc.sync.dma_start(out=gates[1], in_=gate[:, C : 2 * C])
-        for q in range(2, 4):
-            nc.sync.dma_start(out=a_q[q][:], in_=a_planes[:, :, q * HALF : (q + 1) * HALF])
+        load_a(3)
 
         w_src = w2_raw_w[:].bitcast(U16).rearrange("p (m t) -> p t m", t=PACK)
         w_dst = w2_w[:].bitcast(U16).rearrange("p (t m) -> p t m", t=PACK)
@@ -105,23 +106,25 @@ def tile_moe_sdb_relu_kernel(
             nc.vector.tensor_copy(out=w_dst[:, some_planes, :], in_=w_src[:, some_planes, :])
             nc.vector.tensor_copy(out=s_dst[:, some_planes, :], in_=s_src[:, some_planes, :])
 
-        for t in range(PACK):
-            for b in (0, 1) if t == 0 else (1, 0):
-                tokens = slice(b * BANK, (b + 1) * BANK)
-                acc = bank_tile("dc_acc%d%d" % (t, b), t + 1 if b else max(t - 1, 0))
-                nc.tensor.matmul_mx(
-                    out=acc[:],
-                    lhsT=w2_w[:, 2 * P * t : 2 * P * (t + 1)].bitcast(E2M1X4),
-                    lhsT_scale=w2_s[:, P * t : P * (t + 1)],
-                    rhs=dy_w[:, tokens].bitcast(E5M2X4),
-                    rhs_scale=dy_s[:, tokens],
-                    start=True,
-                    stop=True,
-                )
-                if (t, b) == (0, 0):
-                    nc.vector.tensor_copy(out=dc[t][:, tokens], in_=acc[:])
-                else:
-                    nc.scalar.activation(dc[t][:, tokens], acc[:], ACT.Copy)
+        def hidden(t, lo, hi, bank):
+            acc = bank_tile("dc_acc%d_%d" % (t, lo), bank)[:, 0 : hi - lo]
+            nc.tensor.matmul_mx(
+                out=acc,
+                lhsT=w2_w[:, 2 * P * t : 2 * P * (t + 1)].bitcast(E2M1X4),
+                lhsT_scale=w2_s[:, P * t : P * (t + 1)],
+                rhs=dy_w[:, lo:hi].bitcast(E5M2X4),
+                rhs_scale=dy_s[:, lo:hi],
+                start=True,
+                stop=True,
+            )
+            return acc
+
+        for lo, hi, bank in ((0, BANK, 0), (BANK, BANK + HALF, 1)):
+            nc.vector.tensor_copy(out=dc[0][:, lo:hi], in_=hidden(0, lo, hi, bank))
+        nc.scalar.activation(dc[0][:, BANK + HALF : T], hidden(0, BANK + HALF, T, 5), ACT.Copy)
+        for t in range(1, PACK):
+            nc.scalar.activation(dc[t][:, BANK:T], hidden(t, BANK, T, t + 1), ACT.Copy)
+            nc.scalar.activation(dc[t][:, 0:BANK], hidden(t, 0, BANK, t - 1), ACT.Copy)
 
         def entries(lo, hi):
             return offsets[:, lo // PER_COLUMN : hi // PER_COLUMN]
@@ -138,29 +141,30 @@ def tile_moe_sdb_relu_kernel(
         def quantise(q):
             nc.vector.quantize_mx(out=da_w[q][:].bitcast(E5M2X4), scales=da_s[q][:], in_=da[q][:])
 
-        def gather_gated(values, t, lo, hi):
-            nc.vector.tensor_tensor(values, dc[t][:].indirect(entries(lo, hi)), gates[0][:, lo:hi], ALU.mult)
+        def gather_gated(t, h):
+            window = dc[t][:].indirect(entries(h * HALF, (h + 1) * HALF))
+            nc.vector.tensor_tensor(gated[h][:, t, :], window, gate0[h], ALU.mult)
 
-        def gather_high(t, h):
-            gather_gated(gated[h][1][:, t - 2, :], t, h * HALF, (h + 1) * HALF)
+        def weave(engine, q, values, factor):
+            engine.tensor_tensor(woven(da[q][:]), planes(values), planes(factor[:]), ALU.mult)
 
-        pairs = [sb.tile([P, 2, 2 * HALF], BF16, name="pairs0", align_bytes=64)]
-
-        def mask0(h, w):
+        def mask_and_weave(h):
             nc.vector.scalar_tensor_tensor(
-                out=pairs[h][:, w, :].rearrange("p (c e) -> p c e", e=2),
-                in0=a_q[h][:, 2 * w : 2 * w + 2, :].rearrange("p e c -> p c e"),
+                out=da[h][:].rearrange("p (c t) -> p c t", t=PACK),
+                in0=a_q[h][:].rearrange("p t c -> p c t"),
                 scalar=0.0,
-                in1=gated[h][w].rearrange("p e c -> p c e"),
+                in1=gated[h][:].rearrange("p t c -> p c t"),
                 op0=ALU.is_gt,
                 op1=ALU.mult,
             )
 
-        def weave0(h):
-            nc.vector.tensor_copy(
-                out=da[h][:].bitcast(F32).rearrange("p (c w) -> p c w", w=2),
-                in_=pairs[h][:].bitcast(F32).rearrange("p w c -> p c w"),
+        def gate_mask(h, tag):
+            factor = sb.tile([P, PACK, HALF], F32, name="factor%d" % h, tag=tag)
+            rows = gate1[:, half(h)].unsqueeze(1).to_broadcast([P, PACK, HALF])
+            nc.vector.scalar_tensor_tensor(
+                out=factor[:], in0=a_q[2 + h][:], scalar=0.0, in1=rows, op0=ALU.is_gt, op1=ALU.mult
             )
+            return factor
 
         dx = [sb.tile([P, 2, E * C], F32, name="dx%d" % pair) for pair in range(2)]
 
@@ -186,71 +190,57 @@ def tile_moe_sdb_relu_kernel(
         def empty_vector(q, pair):
             nc.vector.tensor_copy(out=dx[pair][:, :, half(q)], in_=expert(q, pair))
 
-        def scatter_scalar(c, q):
-            nc.scalar.activation(res[c][:].indirect(entries(q * HALF, (q + 1) * HALF)), dx[0][:, c, half(q)], ACT.Copy)
+        def scatter_scalar(c, lo, hi):
+            nc.scalar.activation(res[c][:].indirect(entries(lo, hi)), dx[0][:, c, lo:hi], ACT.Copy)
 
-        def scatter_vector(c, first, last):
-            lo, hi = first * HALF, (last + 1) * HALF
+        def scatter_vector(c, lo, hi):
             nc.vector.tensor_copy(res[c][:].indirect(entries(lo, hi)), dx[1][:, c - 2, lo:hi])
 
-        for t in range(2):
-            gather_gated(gated_low[:, t, :], t, 0, C)
-        gather_high(2, 0)
-        mask0(0, 0)
+        for t, h in ((0, 0), (0, 1), (1, 0), (2, 0)):
+            gather_gated(t, h)
         raw1 = sb.tile([P, PACK, C], F32, name="raw1", tag="dy_w", align_bytes=64)
         for t in range(PACK):
             nc.scalar.activation(raw1[:, t, :], dc[t][:].indirect(entries(C, 2 * C)), ACT.Copy)
 
-        def gate_rows(h):
-            return gates[1][:, half(h)].unsqueeze(1).to_broadcast([P, PACK, HALF])
-
-        gather_high(3, 0)
-        gather_high(3, 1)
-        mask0(0, 1)
-        gather_high(2, 1)
-        weave0(0)
-        pairs.append(sb.tile([P, 2, 2 * HALF], BF16, name="pairs1", tag="a0"))
-        mask0(1, 0)
+        factor2 = gate_mask(0, "factor2")
+        for h in range(2):
+            gather_gated(3, h)
+        mask_and_weave(0)
+        gather_gated(2, 1)
         quantise(0)
         for pair in range(2):
             empty_scalar(0, pair)
-        mask0(1, 1)
-        factor2 = sb.tile([P, PACK, HALF], F32, name="factor2", tag="pairs0", align_bytes=64)
-        nc.vector.scalar_tensor_tensor(
-            out=factor2[:], in0=a_q[2][:], scalar=0.0, in1=gate_rows(0), op0=ALU.is_gt, op1=ALU.mult
-        )
-        weave0(1)
-        nc.vector.tensor_tensor(woven(da[2][:]), planes(raw1[:, :, half(0)]), planes(factor2[:]), ALU.mult)
+        gather_gated(1, 1)
+        factor3 = gate_mask(1, "a0")
+        mask_and_weave(1)
+        weave(nc.vector, 2, raw1[:, :, half(0)], factor2)
         quantise(1)
         for c in range(2):
-            scatter_scalar(c, 0)
-        for pair in (1, 0):
+            scatter_scalar(c, 0, HALF)
+        for pair in range(2):
             empty_scalar(1, pair)
-        keep3 = sb.tile([P, PACK, HALF], BF16, name="keep3", tag="a0")
-        nc.vector.tensor_scalar(keep3[:], a_q[3][:], 0.0, None, op0=ALU.is_gt)
         quantise(2)
-        factor3 = sb.tile([P, PACK, HALF], F32, name="factor3", tag="da2", align_bytes=64)
-        nc.gpsimd.tensor_tensor(factor3[:], keep3[:], gate_rows(1), ALU.mult)
-        da.append(sb.tile([P, HALF * PACK], BF16, name="da3", align_bytes=64))
-        nc.gpsimd.tensor_tensor(woven(da[3][:]), planes(raw1[:, :, half(1)]), planes(factor3[:]), ALU.mult)
+        da.append(sb.tile([P, HALF * PACK], BF16, name="da3", tag="da2", align_bytes=64))
+        weave(nc.gpsimd, 3, raw1[:, :, half(1)], factor3)
         res.append(sb.tile([P, T], F32, name="res2", tag="da1", align_bytes=64))
-        scatter_vector(2, 0, 0)
+        scatter_vector(2, 0, HALF)
         for c in range(2):
-            scatter_scalar(c, 1)
+            scatter_scalar(c, HALF, C)
         empty_vector(2, 1)
-        empty_scalar(2, 0)
-        scatter_vector(2, 1, 2)
+        scatter_vector(2, HALF, C)
         quantise(3)
-        res.append(sb.tile([P, T], F32, name="res3", tag="da3", align_bytes=64))
-        for c in range(2):
-            scatter_scalar(c, 2)
-        for pair in (1, 0):
+        res.append(sb.tile([P, T], F32, name="res3", tag="a0"))
+        empty_scalar(2, 0)
+        for pair in range(2):
             empty_scalar(3, pair)
-        scatter_vector(3, 0, 1)
-        scatter_vector(2, 3, 3)
+        scatter_vector(3, 0, C)
+        scatter_scalar(0, C, C + WIDE)
+        scatter_scalar(1, C + WIDE, T)
+        scatter_vector(2, C, T)
         nc.sync.dma_start(out=out[2 * P : 3 * P, :], in_=res[2][:])
-        for c in range(2):
-            scatter_scalar(c, 3)
-            nc.sync.dma_start(out=out[c * P : (c + 1) * P, :], in_=res[c][:])
-        scatter_vector(3, 2, 3)
+        scatter_scalar(0, C + WIDE, T)
+        nc.sync.dma_start(out=out[0:P, :], in_=res[0][:])
+        scatter_scalar(1, C, C + WIDE)
+        nc.sync.dma_start(out=out[P : 2 * P, :], in_=res[1][:])
+        scatter_vector(3, C, T)
         nc.sync.dma_start(out=out[3 * P : 4 * P, :], in_=res[3][:])

from contextlib import ExitStack

import concourse.mybir as mybir

K, T, E, C, H, N = 512, 1024, 2, 512, 512, 512
FLOPS = 2 * N * H * T + 2 * H * K * E * C

F32 = mybir.dt.float32
BF16 = mybir.dt.bfloat16
I32 = mybir.dt.int32
U32 = mybir.dt.uint32
U16 = mybir.dt.uint16
U8 = mybir.dt.uint8
E5M2X4 = mybir.dt.float8_e5m2_x4
E2M1X4 = mybir.dt.float4_e2m1fn_x4
ALU = mybir.AluOpType
ACT = mybir.ActivationFunctionType

P = 128
PACK = 4
QUADS = 4
BANK = 512
HALF = C // 2
WIDE = 384
LINE = 2
PER_COLUMN = 16


def tile_moe_sdb_relu_kernel(
    tc, dy_words, dy_scales, w2t_words, w2t_scales, w1t_words, w1t_scales, a, gate, offs, out
):
    nc = tc.nc
    with ExitStack() as ctx:
        sb = ctx.enter_context(tc.tile_pool(name="sb", bufs=1))
        psum = ctx.enter_context(tc.psum_pool(name="psum", bufs=1))

        def bank_tile(name, first):
            return psum.tile([P, BANK], F32, name=name, offset=first * BANK * 4)

        offsets = sb.tile([P, E * C // PER_COLUMN], U16, name="offsets")
        dy_w = sb.tile([P, T], U32, name="dy_w", align_bytes=64)
        dy_s = sb.tile([P, T], U8, name="dy_s", align_bytes=64)
        w2_raw_w = sb.tile([P, 2 * H], U8, name="w2_raw_w", align_bytes=64)
        w2_raw_s = sb.tile([P, H], U8, name="w2_raw_s", align_bytes=64)
        w2_w = sb.tile([P, 2 * H], U8, name="w2_w", align_bytes=64)
        w2_s = sb.tile([P, H], U8, name="w2_s", align_bytes=64)
        w1_w = sb.tile([P, E, 2 * K], U8, name="w1_w", align_bytes=64)
        w1_s = sb.tile([P, E, K], U8, name="w1_s", align_bytes=64)
        gated = [sb.tile([P, PACK, HALF], F32, name="gated%d" % h) for h in range(2)]
        across = gated[1][:].rearrange("p t c -> p (t c)")[:, HALF + HALF // 2 : 2 * HALF + HALF // 2]
        gate0 = [across, sb.tile([P, HALF], F32, name="gate01")[:]]
        gate1 = sb.tile([P, C], F32, name="gate1")[:]
        a_q = [sb.tile([P, PACK, HALF], F32, name="a%d" % q) for q in range(4)]
        dc = [sb.tile([P, T], F32, name="dc%d" % t) for t in range(PACK)]
        da_w = [sb.tile([P, HALF], U32, name="da_w%d" % q, align_bytes=64) for q in range(4)]
        da_s = [sb.tile([P, HALF], U8, name="da_s%d" % q, align_bytes=64) for q in range(4)]
        da = [sb.tile([P, HALF * PACK], BF16, name="da%d" % q, align_bytes=64) for q in range(3)]
        res = [sb.tile([P, T], F32, name="res%d" % c) for c in range(2)]

        def scale_partitions(q):
            return slice(32 * q, 32 * q + 4)

        def scale_rows(q):
            return slice(4 * q, 4 * q + 4)

        def load_dy_scales(q, queue):
            queue.dma_start(
                out=dy_s[scale_partitions(q), :].bitcast(I32), in_=dy_scales[0, scale_rows(q), :].bitcast(I32)
            )

        w2_rows = w2t_scales[0].bitcast(I32)
        load_dy_scales(0, nc.sync)
        load_dy_scales(1, nc.scalar)
        nc.sync.dma_start(out=w2_raw_s[0:16, :].bitcast(I32), in_=w2_rows)
        nc.scalar.dma_start(out=w2_raw_s[16:128, :].bitcast(I32), in_=w2_rows[2:16, :].partition_broadcast(8))
        nc.sync.dma_start(out=w2_raw_w[:].bitcast(I32), in_=w2t_words[0].bitcast(I32))
        for q in range(2, QUADS):
            load_dy_scales(q, nc.scalar)
        dy_rows = dy_words[0].rearrange("p t d -> p (t d)").bitcast(I32)
        for tokens in (slice(0, BANK), slice(BANK, T)):
            nc.sync.dma_start(out=dy_w[:, tokens].bitcast(I32), in_=dy_rows[:, tokens])
        a_planes = a.rearrange("(p t) j -> p t j", t=PACK)
        nc.sync.dma_start(offsets[:], offs)
        for h in range(2):
            nc.sync.dma_start(out=gate0[h], in_=gate[:, h * HALF : (h + 1) * HALF])

        def load_a(q):
            nc.sync.dma_start(out=a_q[q][:], in_=a_planes[:, :, q * HALF : (q + 1) * HALF])

        nc.sync.dma_start(out=gate1, in_=gate[:, C : 2 * C])
        for q in (2, 0, 1):
            load_a(q)
        nc.sync.dma_start(out=w1_w[:].bitcast(I32), in_=w1t_words[:, 0].rearrange("e p b -> p e b").bitcast(I32))
        for q in range(QUADS):
            nc.sync.dma_start(
                out=w1_s[scale_partitions(q), :, :].bitcast(I32),
                in_=w1t_scales[:, 0, scale_rows(q), :].rearrange("e r k -> r e k").bitcast(I32),
            )
        load_a(3)

        w_src = w2_raw_w[:].bitcast(U16).rearrange("p (m t) -> p t m", t=PACK)
        w_dst = w2_w[:].bitcast(U16).rearrange("p (t m) -> p t m", t=PACK)
        s_src = w2_raw_s[:].rearrange("p (m t) -> p t m", t=PACK)
        s_dst = w2_s[:].rearrange("p (t m) -> p t m", t=PACK)
        for some_planes in (slice(0, 1), slice(1, PACK)):
            nc.vector.tensor_copy(out=w_dst[:, some_planes, :], in_=w_src[:, some_planes, :])
            nc.vector.tensor_copy(out=s_dst[:, some_planes, :], in_=s_src[:, some_planes, :])

        def hidden(t, lo, hi, bank):
            acc = bank_tile("dc_acc%d_%d" % (t, lo), bank)[:, 0 : hi - lo]
            nc.tensor.matmul_mx(
                out=acc,
                lhsT=w2_w[:, 2 * P * t : 2 * P * (t + 1)].bitcast(E2M1X4),
                lhsT_scale=w2_s[:, P * t : P * (t + 1)],
                rhs=dy_w[:, lo:hi].bitcast(E5M2X4),
                rhs_scale=dy_s[:, lo:hi],
                start=True,
                stop=True,
            )
            return acc

        for lo, hi, bank in ((0, BANK, 0), (BANK, BANK + HALF, 1)):
            nc.vector.tensor_copy(out=dc[0][:, lo:hi], in_=hidden(0, lo, hi, bank))
        nc.scalar.activation(dc[0][:, BANK + HALF : T], hidden(0, BANK + HALF, T, 5), ACT.Copy)
        for t in range(1, PACK):
            nc.scalar.activation(dc[t][:, BANK:T], hidden(t, BANK, T, t + 1), ACT.Copy)
            nc.scalar.activation(dc[t][:, 0:BANK], hidden(t, 0, BANK, t - 1), ACT.Copy)

        def entries(lo, hi):
            return offsets[:, lo // PER_COLUMN : hi // PER_COLUMN]

        def half(h):
            return slice(h * HALF, (h + 1) * HALF)

        def woven(ap):
            return ap.rearrange("p (c i t) -> p c t i", i=LINE, t=PACK)

        def planes(ap):
            return ap.rearrange("p t (c i) -> p c t i", i=LINE)

        def quantise(q):
            nc.vector.quantize_mx(out=da_w[q][:].bitcast(E5M2X4), scales=da_s[q][:], in_=da[q][:])

        def gather_gated(t, h):
            window = dc[t][:].indirect(entries(h * HALF, (h + 1) * HALF))
            nc.vector.tensor_tensor(gated[h][:, t, :], window, gate0[h], ALU.mult)

        def weave(engine, q, values, factor):
            engine.tensor_tensor(woven(da[q][:]), planes(values), planes(factor[:]), ALU.mult)

        def mask_and_weave(h):
            nc.vector.scalar_tensor_tensor(
                out=da[h][:].rearrange("p (c t) -> p c t", t=PACK),
                in0=a_q[h][:].rearrange("p t c -> p c t"),
                scalar=0.0,
                in1=gated[h][:].rearrange("p t c -> p c t"),
                op0=ALU.is_gt,
                op1=ALU.mult,
            )

        def gate_mask(h, tag):
            factor = sb.tile([P, PACK, HALF], F32, name="factor%d" % h, tag=tag)
            rows = gate1[:, half(h)].unsqueeze(1).to_broadcast([P, PACK, HALF])
            nc.vector.scalar_tensor_tensor(
                out=factor[:], in0=a_q[2 + h][:], scalar=0.0, in1=rows, op0=ALU.is_gt, op1=ALU.mult
            )
            return factor

        dx = [sb.tile([P, 2, E * C], F32, name="dx%d" % pair) for pair in range(2)]

        def expert(q, pair):
            e = q // 2
            acc = bank_tile("dx_acc%d%d" % (q, pair), (5 + 2 * q + pair) % 8)
            for j in range(2):
                c = 2 * pair + j
                nc.tensor.matmul_mx(
                    out=acc[:, half(j)],
                    lhsT=w1_w[:, e, 2 * P * c : 2 * P * (c + 1)].bitcast(E2M1X4),
                    lhsT_scale=w1_s[:, e, P * c : P * (c + 1)],
                    rhs=da_w[q][:].bitcast(E5M2X4),
                    rhs_scale=da_s[q][:],
                    start=True,
                    stop=True,
                )
            return acc[:].rearrange("p (j s) -> p j s", j=2)

        def empty_scalar(q, pair):
            nc.scalar.copy(out=dx[pair][:, :, half(q)], in_=expert(q, pair))

        def empty_vector(q, pair):
            nc.vector.tensor_copy(out=dx[pair][:, :, half(q)], in_=expert(q, pair))

        def scatter_scalar(c, lo, hi):
            nc.scalar.activation(res[c][:].indirect(entries(lo, hi)), dx[0][:, c, lo:hi], ACT.Copy)

        def scatter_vector(c, lo, hi):
            nc.vector.tensor_copy(res[c][:].indirect(entries(lo, hi)), dx[1][:, c - 2, lo:hi])

        for t, h in ((0, 0), (0, 1), (1, 0), (2, 0)):
            gather_gated(t, h)
        raw1 = sb.tile([P, PACK, C], F32, name="raw1", tag="dy_w", align_bytes=64)
        for t in range(PACK):
            nc.scalar.activation(raw1[:, t, :], dc[t][:].indirect(entries(C, 2 * C)), ACT.Copy)

        factor2 = gate_mask(0, "factor2")
        for h in range(2):
            gather_gated(3, h)
        mask_and_weave(0)
        gather_gated(2, 1)
        quantise(0)
        for pair in range(2):
            empty_scalar(0, pair)
        gather_gated(1, 1)
        factor3 = gate_mask(1, "a0")
        mask_and_weave(1)
        weave(nc.vector, 2, raw1[:, :, half(0)], factor2)
        quantise(1)
        for c in range(2):
            scatter_scalar(c, 0, HALF)
        for pair in range(2):
            empty_scalar(1, pair)
        quantise(2)
        da.append(sb.tile([P, HALF * PACK], BF16, name="da3", tag="da2", align_bytes=64))
        weave(nc.gpsimd, 3, raw1[:, :, half(1)], factor3)
        res.append(sb.tile([P, T], F32, name="res2", tag="da1", align_bytes=64))
        scatter_vector(2, 0, HALF)
        for c in range(2):
            scatter_scalar(c, HALF, C)
        empty_vector(2, 1)
        scatter_vector(2, HALF, C)
        quantise(3)
        res.append(sb.tile([P, T], F32, name="res3", tag="a0"))
        empty_scalar(2, 0)
        for pair in range(2):
            empty_scalar(3, pair)
        scatter_vector(3, 0, C)
        scatter_scalar(0, C, C + WIDE)
        scatter_scalar(1, C + WIDE, T)
        scatter_vector(2, C, T)
        nc.sync.dma_start(out=out[2 * P : 3 * P, :], in_=res[2][:])
        scatter_scalar(0, C + WIDE, T)
        nc.sync.dma_start(out=out[0:P, :], in_=res[0][:])
        scatter_scalar(1, C, C + WIDE)
        nc.sync.dma_start(out=out[P : 2 * P, :], in_=res[1][:])
        scatter_vector(3, C, T)
        nc.sync.dma_start(out=out[3 * P : 4 * P, :], in_=res[3][:])
